import numpy as np
import ml_dtypes


def mxq(x, axis, fmt="e4m3"):
    dtype, down = {"e4m3": (ml_dtypes.float8_e4m3fn, 7), "e5m2": (ml_dtypes.float8_e5m2, 14)}[fmt]
    v = np.moveaxis(np.asarray(x, np.float32).astype(ml_dtypes.bfloat16).astype(np.float64), axis, -1)
    blocks = v.reshape(v.shape[:-1] + (-1, 32))
    amax = np.abs(blocks).max(-1, keepdims=True)
    byte = np.maximum(np.where(amax > 0, np.frexp(amax)[1] - 1 + 127, 0) - down, 1)
    scale = np.exp2(byte - 127.0)
    codes = (blocks / scale).astype(np.float32).astype(dtype).astype(np.float64)
    return np.moveaxis((codes * scale).reshape(v.shape), -1, axis)


WIDE = False


def mx_kscale(k):
    if not WIDE:
        return np.ones(k)
    levels = np.array([10, -10, 5, -5, 0])
    if k % 512:
        return np.exp2(np.random.permutation(np.resize(levels, k // 32))).repeat(32)
    a = np.empty((k // 512, 16))
    for p in range(k // 512):
        a[p, :8] = np.random.permutation(np.resize(levels, 8))
        for g in range(8):
            far = levels[np.abs(levels - a[p, g]) >= 10]
            a[p, g + 8] = far[np.random.randint(len(far))]
    return np.exp2(a.ravel()).repeat(32)


BF16 = ml_dtypes.bfloat16


def bf(x):
    return np.asarray(x, np.float32).astype(BF16)


def f64(x):
    return np.asarray(x).astype(np.float64)


E2M1 = np.array([0.0, 0.5, 1.0, 1.5, 2.0, 3.0, 4.0, 6.0, -0.0, -0.5, -1.0, -1.5, -2.0, -3.0, -4.0, -6.0])


def pack_weight(w, fmt):
    k, n = w.shape
    w = f64(bf(w)).reshape(k // 32, 32, n)
    amax = np.abs(w).max(1)
    if fmt == "e4m3":
        byte = np.frexp(amax)[1] - 1 + 127 - 7
    else:
        mant, ex = np.frexp(amax / 6.0)
        byte = np.where(mant > 0.5, ex, ex - 1) + 127
    byte = np.clip(np.where(amax > 0, byte, 1), 1, 254)
    scaled = (w * np.exp2(127.0 - byte)[:, None, :]).reshape(k, n).astype(np.float32)
    by_word = np.ascontiguousarray(scaled.reshape(k // 512, 128, 4, n).transpose(0, 1, 3, 2))
    if fmt == "e4m3":
        words = by_word.astype(ml_dtypes.float8_e4m3fn).view(np.uint8)
    else:
        c = by_word.astype(ml_dtypes.float4_e2m1fn).view(np.uint8) & 0xF
        words = c[..., 0::2] | (c[..., 1::2] << 4)
    return np.ascontiguousarray(words), np.ascontiguousarray(byte.astype(np.uint8).reshape(k // 512, 16, n))


def unpack_weight(words, scales, fmt):
    g, p, n, _ = words.shape
    if fmt == "e4m3":
        vals = np.ascontiguousarray(words).view(ml_dtypes.float8_e4m3fn).astype(np.float64)
    else:
        nib = np.empty((g, p, n, 4), np.uint8)
        nib[..., 0::2] = words & 0xF
        nib[..., 1::2] = words >> 4
        vals = E2M1[nib]
    vals = vals * np.repeat(np.exp2(scales.astype(np.float64) - 127.0), 8, axis=1)[..., None]
    return vals.transpose(0, 1, 3, 2).reshape(g * 512, n)
def pack4(w):
    words, scales = pack_weight(w, "e2m1")
    return words.reshape(words.shape[0], 128, -1), scales


def unpack4(words, scales):
    return unpack_weight(words.reshape(words.shape[0], 128, -1, 2), scales, "e2m1")


M, KL, KT, N = 1024, 512, 1536, 2048


def setup_inputs():
    s = mx_kscale(KL)
    t = mx_kscale(KT)
    c_lead = np.random.standard_normal((M, KL)) * s
    a_lead = np.random.standard_normal((KL, N)) / np.sqrt(KL) / s[:, None]
    c_tail = 0.5 * np.random.standard_normal((M, KT)) * t
    a_tail = np.random.standard_normal((KT, N)) / np.sqrt(KT) / t[:, None]
    a_tail_words, a_tail_scales = pack4(a_tail)
    return {"c_lead": bf(c_lead),
            "c_tail": bf(c_tail),
            "a_lead": bf(a_lead),
            "a_tail_words": a_tail_words,
            "a_tail_scales": a_tail_scales,
            "kappa": bf(np.exp(0.3 * np.random.standard_normal(M))),
            "load": bf(np.random.standard_normal(N)),
            "dinv": bf(1 + 0.1 * np.random.standard_normal(N))}


def reference(c_lead, c_tail, a_lead, a_tail_words, a_tail_scales, kappa, load, dinv):
    a_tail = unpack4(a_tail_words, a_tail_scales)
    lead = mxq(f64(c_lead), 1, "e4m3") @ mxq(f64(a_lead), 0, "e4m3")
    tail = mxq(f64(c_tail), 1, "e4m3") @ a_tail
    au = lead + tail
    return (f64(load) - f64(kappa)[:, None] * au) * f64(dinv)

@@ -1,0 +1,344 @@
+from contextlib import ExitStack
+
+import concourse.mybir as mybir
+from concourse.masks import make_identity
+
+M, KL, KT, N = 1024, 512, 1536, 2048
+FLOPS = 2 * M * (KL + KT) * N
+
+F32 = mybir.dt.float32
+BF16 = mybir.dt.bfloat16
+I32 = mybir.dt.int32
+U32 = mybir.dt.uint32
+U8 = mybir.dt.uint8
+FP8X4 = mybir.dt.float8_e4m3fn_x4
+FP4X4 = mybir.dt.float4_e2m1fn_x4
+ALU = mybir.AluOpType
+
+P = 128
+PACK = 4
+K_PASS = P * PACK
+ROWS = M // P
+N_TILE = 512
+CHUNKS = N // N_TILE
+HALF = N // 2
+TAIL_PASSES = KT // K_PASS
+LEAD = TAIL_PASSES
+PASSES = TAIL_PASSES + 1
+
+
+def tile_reduced_basis_jacobi_residual_s1_kernel(
+    tc, c_lead, c_tail, a_lead, a_tail_words, a_tail_scales, kappa, load, dinv, out
+):
+    nc = tc.nc
+    c_lead_rows = c_lead.rearrange("(p i) k -> p i k", i=ROWS)
+    c_tail_rows = c_tail.rearrange("(p i) k -> p i k", i=ROWS)
+    out_rows = out.rearrange("(p i) n -> p i n", i=ROWS)
+    a_lead_rows = a_lead.rearrange("(p j) n -> p j n", j=PACK)
+    tail_words = a_tail_words.rearrange("g p b -> p g b")
+    tail_scale_rows = a_tail_scales.rearrange("g (q r) n -> r q g n", r=4)
+
+    with ExitStack() as ctx:
+        keep = ctx.enter_context(tc.tile_pool(name="keep", bufs=1))
+        stage = ctx.enter_context(tc.tile_pool(name="stage", bufs=3))
+        psum = ctx.enter_context(tc.psum_pool(name="psum", bufs=1))
+        ctx.enter_context(tc.manual_schedule())
+
+        c_words = {}
+        c_mx = {}
+        a_mx = {}
+        a_lead_raw = {}
+        a_lead_grouped = {}
+        tail_planes = {}
+        load_wide = {}
+        dinv_wide = {}
+        acc = {}
+        result = {}
+
+        def load_c_tail(m):
+            raw = keep.tile([P, KT], BF16, name="c_tail_%d" % m, align_bytes=64)
+            nc.sync.dma_start(out=raw[:], in_=c_tail_rows[:, m, :])
+            words = raw[:].bitcast(F32)
+            for g in range(TAIL_PASSES):
+                c_words[m, g] = words[:, 256 * g : 256 * (g + 1)]
+
+        def load_c_lead(m):
+            raw = keep.tile([P, 2 * KL], BF16, name="c_lead_%d" % m, align_bytes=64)
+            nc.sync.dma_start(
+                out=raw[:], in_=c_lead_rows[:, m : m + 2, :].rearrange("p i k -> p (i k)")
+            )
+            words = raw[:].bitcast(F32)
+            for i in range(2):
+                c_words[m + i, LEAD] = words[:, 256 * i : 256 * (i + 1)]
+
+        def load_a_lead(n):
+            raw = keep.tile([P, PACK, N_TILE], BF16, name="a_lead_%d" % n, align_bytes=64)
+            nc.sync.dma_start(out=raw[:], in_=a_lead_rows[:, :, n * N_TILE : (n + 1) * N_TILE])
+            a_lead_raw[n] = raw
+
+        def clear_tail_scales(half):
+            plane = keep.tile([P, TAIL_PASSES, HALF], U8, name="tail_scales_%d" % half, align_bytes=64)
+            nc.vector.memset(plane[:].rearrange("p g n -> p (g n)").bitcast(I32), 0)
+            tail_planes[half] = plane
+
+        def load_tail_scales(half):
+            cols = slice(half * HALF, (half + 1) * HALF)
+            for r in range(4):
+                nc.sync.dma_start(
+                    out=tail_planes[half][r:P:32, :, :].bitcast(I32),
+                    in_=tail_scale_rows[r][:, :, cols].bitcast(I32),
+                )
+
+        def load_tail_words(half, passes):
+            first, count = passes[0], len(passes)
+            codes = keep.tile([P, count, 2 * HALF], U8, name="tail_words_%d_%d" % (half, first), align_bytes=64)
+            nc.sync.dma_start(
+                out=codes[:].bitcast(I32),
+                in_=tail_words[:, first : first + count, 2 * half * HALF : 2 * (half + 1) * HALF].bitcast(I32),
+            )
+            for g in passes:
+                for j in range(2):
+                    a_mx[g, 2 * half + j] = (
+                        codes[:, g - first, 2 * j * N_TILE : 2 * (j + 1) * N_TILE].bitcast(FP4X4),
+                        tail_planes[half][:, g, j * N_TILE : (j + 1) * N_TILE],
+                    )
+
+        def turn(items):
+            bank = psum.tile([P, 2 * len(items), P], F32, name="turned", tag="turned", bufs=3)
+            for s, item in enumerate(items):
+                for u in range(2):
+                    nc.tensor.transpose(bank[:, 2 * s + u, :], c_words[item][:, u:256:2], identity[:])
+            return bank
+
+        def new_grouped(count):
+            grouped = stage.tile([P, count * K_PASS], BF16, name="c_grouped", tag="c_grouped", align_bytes=64)
+            return grouped
+
+        def copy_turned(bank, grouped, first):
+            count = bank.shape[1] // 2
+            words = grouped[:, first * K_PASS : (first + count) * K_PASS].bitcast(F32)
+            nc.scalar.copy(
+                out=words.rearrange("p (s r u) -> p s r u", s=count, u=2),
+                in_=bank[:].rearrange("p (s u) r -> p s r u", u=2),
+            )
+
+        def quantize_c(items, grouped):
+            name = "%d_%d" % items[0]
+            codes = keep.tile([P, len(items) * P], U32, name="c_codes_" + name, align_bytes=64)
+            scales = keep.tile([P, len(items) * P], U8, name="c_scales_" + name, align_bytes=64)
+            nc.vector.quantize_mx(out=codes[:].bitcast(FP8X4), scales=scales[:], in_=grouped[:])
+            for s, item in enumerate(items):
+                cols = slice(s * P, (s + 1) * P)
+                c_mx[item] = (codes[:, cols].bitcast(FP8X4), scales[:, cols])
+
+        def group_a_lead(n, copy):
+            grouped = keep.tile([P, N_TILE, PACK], BF16, name="a_grouped_%d" % n, align_bytes=64)
+            copy(
+                out=grouped[:].rearrange("p (c i) t -> p c t i", i=4),
+                in_=a_lead_raw[n][:].rearrange("p t (c i) -> p c t i", i=4),
+            )
+            a_lead_grouped[n] = grouped
+
+        def quantize_a_lead(n):
+            codes = keep.tile([P, N_TILE], U32, name="a_codes_%d" % n, align_bytes=64)
+            scales = keep.tile([P, N_TILE], U8, name="a_scales_%d" % n, align_bytes=64)
+            nc.vector.quantize_mx(
+                out=codes[:].bitcast(FP8X4),
+                scales=scales[:],
+                in_=a_lead_grouped[n][:].rearrange("p c t -> p (c t)"),
+            )
+            a_mx[LEAD, n] = (codes[:].bitcast(FP8X4), scales[:])
+
+        def spread(n, tag, bufs):
+            bank = psum.tile([P, 4, P], F32, name=tag, tag=tag, bufs=bufs)
+            for c in range(4):
+                column = pair_words[:, 4 * n + c : 4 * n + c + 1].to_broadcast([P, P])
+                nc.tensor.transpose(bank[:, c, :], column, identity[:])
+            return bank[:].rearrange("q c p -> q (c p)").bitcast(BF16).rearrange("q (c p e) -> q e p c", c=4, e=2)
+
+        def copy_spread(n, pairs, which, table, name):
+            wide = keep.tile([P, N_TILE], F32, name="%s_%d" % (name, n))
+            nc.scalar.copy(out=wide[:].rearrange("q (p c) -> q p c", c=4), in_=pairs[:, which])
+            table[n] = wide[:].rearrange("q (p c) -> q p c", c=4)
+
+        def multiply(m, n, g):
+            if g == 0:
+                acc[m, n] = psum.tile([P, N_TILE], F32, name="acc", tag="acc", bufs=5)
+            nc.tensor.matmul_mx(
+                out=acc[m, n][:],
+                lhsT=c_mx[m, g][0],
+                lhsT_scale=c_mx[m, g][1],
+                rhs=a_mx[g, n][0],
+                rhs_scale=a_mx[g, n][1],
+                start=(g == 0),
+                stop=(g == LEAD),
+            )
+
+        def multiply_block(m, n):
+            for g in range(PASSES):
+                multiply(m, n, g)
+
+        def result_cols(m, n):
+            half, j = divmod(n, 2)
+            if (m, half) not in result:
+                result[m, half] = keep.tile([P, HALF], F32, name="result_%d_%d" % (m, half))
+            return result[m, half][:, j * N_TILE : (j + 1) * N_TILE]
+
+        def residual(m, n):
+            nc.vector.scalar_tensor_tensor(
+                out=result_cols(m, n),
+                in0=acc[m, n][:],
+                scalar=neg_kappa[:, m : m + 1],
+                in1=load_wide[n].rearrange("q p c -> q (p c)"),
+                op0=ALU.mult,
+                op1=ALU.add,
+            )
+
+        def scale(m, n, engine):
+            cols = result_cols(m, n).rearrange("q (p c) -> q p c", c=4)
+            engine.tensor_tensor(out=cols, in0=cols, in1=dinv_wide[n], op=ALU.mult)
+
+        def store(m, half):
+            nc.sync.dma_start(out=out_rows[:, m, half * HALF : (half + 1) * HALF], in_=result[m, half][:])
+
+        def store_block(m, n):
+            nc.sync.dma_start(out=out_rows[:, m, n * N_TILE : (n + 1) * N_TILE], in_=result_cols(m, n))
+
+        clear_tail_scales(0)
+        identity = keep.tile([P, P], F32)
+        make_identity(nc, identity[:])
+        load_in = keep.tile([P, CHUNKS, 4], BF16)
+        dinv_in = keep.tile([P, CHUNKS, 4], BF16)
+        kappa_in = keep.tile([P, ROWS], BF16)
+        load_c_tail(0)
+        nc.scalar.dma_start(out=load_in[:], in_=load.rearrange("(h p c) -> p h c", h=CHUNKS, c=4))
+        nc.scalar.dma_start(out=dinv_in[:], in_=dinv.rearrange("(h p c) -> p h c", h=CHUNKS, c=4))
+        nc.gpsimd.dma_start(out=kappa_in[:], in_=kappa.rearrange("(p i) -> p i", i=ROWS))
+        load_tail_scales(0)
+        clear_tail_scales(1)
+        for g in range(TAIL_PASSES):
+            load_tail_words(0, [g])
+        load_c_tail(1)
+        load_c_lead(0)
+        load_a_lead(0)
+        load_a_lead(1)
+        load_c_tail(2)
+        load_c_lead(2)
+        load_c_tail(3)
+        load_c_tail(4)
+        load_c_lead(4)
+        load_a_lead(2)
+        load_c_tail(5)
+        load_a_lead(3)
+        load_c_tail(6)
+        load_c_lead(6)
+        load_c_tail(7)
+        load_tail_scales(1)
+        load_tail_words(1, list(range(TAIL_PASSES)))
+
+        pairs_in = keep.tile([P, 4 * CHUNKS, 2], BF16)
+        nc.vector.tensor_copy(out=pairs_in[:, :, 0], in_=load_in[:].rearrange("p h c -> p (h c)"))
+        nc.vector.tensor_copy(out=pairs_in[:, :, 1], in_=dinv_in[:].rearrange("p h c -> p (h c)"))
+        pair_words = pairs_in[:].rearrange("p a e -> p (a e)").bitcast(F32)
+
+        def prepare(items):
+            bank = turn(items)
+            grouped = new_grouped(len(items))
+            copy_turned(bank, grouped, 0)
+            return grouped
+
+        def prepare_row(m):
+            banks = [turn([(m, 0), (m, 1)]), turn([(m, 2), (m, LEAD)])]
+            grouped = new_grouped(PASSES)
+            copy_turned(banks[0], grouped, 0)
+            copy_turned(banks[1], grouped, 2)
+            return grouped
+
+        def spread_both(n, tag, bufs):
+            pairs = spread(n, tag, bufs)
+            copy_spread(n, pairs, 0, load_wide, "load_wide")
+            copy_spread(n, pairs, 1, dinv_wide, "dinv_wide")
+
+        def row_items(m):
+            return [(m, g) for g in range(PASSES)]
+
+        for items in ([(0, 0), (0, 1)], [(0, 2)]):
+            quantize_c(items, prepare(items))
+        spread_both(0, "acc", 5)
+        for g in (0, 1):
+            for n in (0, 1):
+                multiply(0, n, g)
+        for items in ([(1, 0), (1, 1)], [(1, 2)]):
+            quantize_c(items, prepare(items))
+        lead_items = [(0, LEAD), (1, LEAD)]
+        lead_grouped = prepare(lead_items)
+        spread_both(1, "acc", 5)
+        for n in (0, 1):
+            multiply(0, n, 2)
+        for g in range(TAIL_PASSES):
+            for n in (0, 1):
+                multiply(1, n, g)
+        neg_kappa = keep.tile([P, ROWS], F32)
+        group_a_lead(0, nc.vector.tensor_copy)
+        quantize_c(lead_items, lead_grouped)
+        quantize_a_lead(0)
+        group_a_lead(1, nc.vector.tensor_copy)
+        nc.vector.tensor_scalar(out=neg_kappa[:], in0=kappa_in[:], scalar1=-1.0, scalar2=None, op0=ALU.mult)
+        quantize_a_lead(1)
+        quantize_c(row_items(2), prepare_row(2))
+        for n in (0, 1):
+            for m in (0, 1):
+                multiply(m, n, LEAD)
+        residual(0, 0)
+        residual(1, 0)
+        residual(0, 1)
+
+        for m in range(2, ROWS):
+            ahead = m + 1
+            if ahead < ROWS:
+                grouped = prepare_row(ahead)
+            if ahead == ROWS - 2:
+                spread_both(2, "turned", 3)
+            if ahead == ROWS - 1:
+                pairs = spread(3, "turned", 3)
+                copy_spread(3, pairs, 0, load_wide, "load_wide")
+                dinv_wide[3] = pairs[:, 1]
+            if m in (3, 4):
+                group_a_lead(m - 1, nc.scalar.copy)
+            residual(m - 1, 1)
+            multiply_block(m, 0)
+            if m > 2:
+                scale(m - 2, 0, nc.vector)
+                scale(m - 2, 1, nc.vector)
+                store(m - 2, 0)
+            if ahead < ROWS:
+                quantize_c(row_items(ahead), grouped)
+            residual(m, 0)
+            if m == 2:
+                scale(0, 0, nc.vector)
+                scale(0, 1, nc.vector)
+                store(0, 0)
+            if m in (4, 5):
+                quantize_a_lead(m - 2)
+            multiply_block(m, 1)
+        last = ROWS - 1
+        scale(last - 1, 0, nc.vector)
+        scale(last - 1, 1, nc.vector)
+        store(last - 1, 0)
+        residual(last, 1)
+        scale(last, 0, nc.vector)
+        scale(last, 1, nc.gpsimd)
+        store(last, 0)
+
+        for m in range(ROWS):
+            multiply_block(m, 2)
+            residual(m, 2)
+            scale(m, 2, nc.gpsimd)
+            if m > 0:
+                scale(m - 1, 3, nc.vector)
+                store(m - 1, 1)
+            multiply_block(m, 3)
+            residual(m, 3)
+        store_block(last, 2)
+        scale(last, 3, nc.vector)
+        store_block(last, 3)

@@ -25,6 +25,7 @@ HALF = N // 2
 TAIL_PASSES = KT // K_PASS
 LEAD = TAIL_PASSES
 PASSES = TAIL_PASSES + 1
+SPLIT = 512
 
 
 def tile_reduced_basis_jacobi_residual_s1_kernel(
@@ -44,12 +45,14 @@ def tile_reduced_basis_jacobi_residual_s1_kernel(
         psum = ctx.enter_context(tc.psum_pool(name="psum", bufs=1))
         ctx.enter_context(tc.manual_schedule())
 
+        c_raw = {}
         c_words = {}
         c_mx = {}
         a_mx = {}
         a_lead_raw = {}
         a_lead_grouped = {}
         tail_planes = {}
+        tail_scale = {}
         load_wide = {}
         dinv_wide = {}
         acc = {}
@@ -58,56 +61,69 @@ def tile_reduced_basis_jacobi_residual_s1_kernel(
         def load_c_tail(m):
             raw = keep.tile([P, KT], BF16, name="c_tail_%d" % m, align_bytes=64)
             nc.sync.dma_start(out=raw[:], in_=c_tail_rows[:, m, :])
-            words = raw[:].bitcast(F32)
-            for g in range(TAIL_PASSES):
-                c_words[m, g] = words[:, 256 * g : 256 * (g + 1)]
+            c_raw[m, "tail"] = (raw[:].bitcast(F32), [(m, g) for g in range(TAIL_PASSES)])
 
         def load_c_lead(m):
             raw = keep.tile([P, 2 * KL], BF16, name="c_lead_%d" % m, align_bytes=64)
             nc.sync.dma_start(
                 out=raw[:], in_=c_lead_rows[:, m : m + 2, :].rearrange("p i k -> p (i k)")
             )
-            words = raw[:].bitcast(F32)
-            for i in range(2):
-                c_words[m + i, LEAD] = words[:, 256 * i : 256 * (i + 1)]
+            c_raw[m, "lead"] = (raw[:].bitcast(F32), [(m, LEAD), (m + 1, LEAD)])
+
+        def take_stepped(key):
+            words, items = c_raw[key]
+            for s, item in enumerate(items):
+                c_words[item] = [words[:, 2 * P * s + u : 2 * P * (s + 1) : 2] for u in range(2)]
+
+        def sort_words(key):
+            words, items = c_raw[key]
+            ordered = keep.tile([P, 2, len(items) * P], F32, name="c_sorted_" + key[1], tag="c_sorted_" + key[1], bufs=2)
+            nc.scalar.copy(
+                out=ordered[:].rearrange("p u (b i) -> p b u i", i=4),
+                in_=words.rearrange("p (b i u) -> p b u i", i=4, u=2),
+            )
+            for s, item in enumerate(items):
+                c_words[item] = [ordered[:, u, P * s : P * (s + 1)] for u in range(2)]
 
         def load_a_lead(n):
             raw = keep.tile([P, PACK, N_TILE], BF16, name="a_lead_%d" % n, align_bytes=64)
             nc.sync.dma_start(out=raw[:], in_=a_lead_rows[:, :, n * N_TILE : (n + 1) * N_TILE])
             a_lead_raw[n] = raw
 
-        def clear_tail_scales(half):
-            plane = keep.tile([P, TAIL_PASSES, HALF], U8, name="tail_scales_%d" % half, align_bytes=64)
+        def clear_tail_scales(first, count):
+            plane = keep.tile([P, TAIL_PASSES, count * N_TILE], U8, name="tail_scales_%d" % first, align_bytes=64)
             nc.vector.memset(plane[:].rearrange("p g n -> p (g n)").bitcast(I32), 0)
-            tail_planes[half] = plane
+            tail_planes[first] = plane
 
-        def load_tail_scales(half):
-            cols = slice(half * HALF, (half + 1) * HALF)
+        def load_tail_scales(first, count):
+            cols = slice(first * N_TILE, (first + count) * N_TILE)
             for r in range(4):
                 nc.sync.dma_start(
-                    out=tail_planes[half][r:P:32, :, :].bitcast(I32),
+                    out=tail_planes[first][r:P:32, :, :].bitcast(I32),
                     in_=tail_scale_rows[r][:, :, cols].bitcast(I32),
                 )
+            for j in range(count):
+                for g in range(TAIL_PASSES):
+                    tail_scale[g, first + j] = tail_planes[first][:, g, j * N_TILE : (j + 1) * N_TILE]
 
-        def load_tail_words(half, passes):
-            first, count = passes[0], len(passes)
-            codes = keep.tile([P, count, 2 * HALF], U8, name="tail_words_%d_%d" % (half, first), align_bytes=64)
-            nc.sync.dma_start(
-                out=codes[:].bitcast(I32),
-                in_=tail_words[:, first : first + count, 2 * half * HALF : 2 * (half + 1) * HALF].bitcast(I32),
+        def load_tail_words(first, count, passes):
+            codes = keep.tile(
+                [P, len(passes), 2 * count * N_TILE], U8, name="tail_words_%d_%d" % (first, passes[0]), align_bytes=64
             )
-            for g in passes:
-                for j in range(2):
-                    a_mx[g, 2 * half + j] = (
-                        codes[:, g - first, 2 * j * N_TILE : 2 * (j + 1) * N_TILE].bitcast(FP4X4),
-                        tail_planes[half][:, g, j * N_TILE : (j + 1) * N_TILE],
-                    )
+            cols = slice(2 * first * N_TILE, 2 * (first + count) * N_TILE)
+            nc.sync.dma_start(
+                out=codes[:].bitcast(I32), in_=tail_words[:, passes[0] : passes[-1] + 1, cols].bitcast(I32)
+            )
+            for s, g in enumerate(passes):
+                for j in range(count):
+                    words = codes[:, s, 2 * j * N_TILE : 2 * (j + 1) * N_TILE].bitcast(FP4X4)
+                    a_mx[g, first + j] = (words, tail_scale[g, first + j])
 
-        def turn(items):
-            bank = psum.tile([P, 2 * len(items), P], F32, name="turned", tag="turned", bufs=3)
+        def turn(items, tag):
+            bank = psum.tile([P, 2 * len(items), P], F32, name="turned", tag=tag)
             for s, item in enumerate(items):
                 for u in range(2):
-                    nc.tensor.transpose(bank[:, 2 * s + u, :], c_words[item][:, u:256:2], identity[:])
+                    nc.tensor.transpose(bank[:, 2 * s + u, :], c_words[item][u], identity[:])
             return bank
 
         def new_grouped(count):
@@ -131,13 +147,13 @@ def tile_reduced_basis_jacobi_residual_s1_kernel(
                 cols = slice(s * P, (s + 1) * P)
                 c_mx[item] = (codes[:, cols].bitcast(FP8X4), scales[:, cols])
 
-        def group_a_lead(n, copy):
-            grouped = keep.tile([P, N_TILE, PACK], BF16, name="a_grouped_%d" % n, align_bytes=64)
+        def group_a_lead(n, copy, first=0, last=N_TILE):
+            if n not in a_lead_grouped:
+                a_lead_grouped[n] = keep.tile([P, N_TILE, PACK], BF16, name="a_grouped_%d" % n, align_bytes=64)
             copy(
-                out=grouped[:].rearrange("p (c i) t -> p c t i", i=4),
-                in_=a_lead_raw[n][:].rearrange("p t (c i) -> p c t i", i=4),
+                out=a_lead_grouped[n][:, first:last, :].rearrange("p (c i) t -> p c t i", i=4),
+                in_=a_lead_raw[n][:, :, first:last].rearrange("p t (c i) -> p c t i", i=4),
             )
-            a_lead_grouped[n] = grouped
 
         def quantize_a_lead(n):
             codes = keep.tile([P, N_TILE], U32, name="a_codes_%d" % n, align_bytes=64)
@@ -149,8 +165,8 @@ def tile_reduced_basis_jacobi_residual_s1_kernel(
             )
             a_mx[LEAD, n] = (codes[:].bitcast(FP8X4), scales[:])
 
-        def spread(n, tag, bufs):
-            bank = psum.tile([P, 4, P], F32, name=tag, tag=tag, bufs=bufs)
+        def spread(n, tag):
+            bank = psum.tile([P, 4, P], F32, name="spread", tag=tag)
             for c in range(4):
                 column = pair_words[:, 4 * n + c : 4 * n + c + 1].to_broadcast([P, P])
                 nc.tensor.transpose(bank[:, c, :], column, identity[:])
@@ -161,9 +177,15 @@ def tile_reduced_basis_jacobi_residual_s1_kernel(
             nc.scalar.copy(out=wide[:].rearrange("q (p c) -> q p c", c=4), in_=pairs[:, which])
             table[n] = wide[:].rearrange("q (p c) -> q p c", c=4)
 
+        def acc_tag(m, n):
+            if (m, n) == (2, 0):
+                return "spare"
+            order = m + 2 * n if m < 2 and n < 2 else 2 * m + n % 2 - 1 + (2 * ROWS if n > 1 else 0)
+            return "acc_%d" % (order % 4)
+
         def multiply(m, n, g):
             if g == 0:
-                acc[m, n] = psum.tile([P, N_TILE], F32, name="acc", tag="acc", bufs=5)
+                acc[m, n] = psum.tile([P, N_TILE], F32, name="acc", tag=acc_tag(m, n))
             nc.tensor.matmul_mx(
                 out=acc[m, n][:],
                 lhsT=c_mx[m, g][0],
@@ -184,19 +206,19 @@ def tile_reduced_basis_jacobi_residual_s1_kernel(
                 result[m, half] = keep.tile([P, HALF], F32, name="result_%d_%d" % (m, half))
             return result[m, half][:, j * N_TILE : (j + 1) * N_TILE]
 
-        def residual(m, n):
+        def residual(m, n, bank, first, width):
             nc.vector.scalar_tensor_tensor(
-                out=result_cols(m, n),
-                in0=acc[m, n][:],
+                out=result_cols(m, n)[:, first : first + width],
+                in0=bank,
                 scalar=neg_kappa[:, m : m + 1],
-                in1=load_wide[n].rearrange("q p c -> q (p c)"),
+                in1=load_wide[n].rearrange("q p c -> q (p c)")[:, first : first + width],
                 op0=ALU.mult,
                 op1=ALU.add,
             )
 
-        def scale(m, n, engine):
-            cols = result_cols(m, n).rearrange("q (p c) -> q p c", c=4)
-            engine.tensor_tensor(out=cols, in0=cols, in1=dinv_wide[n], op=ALU.mult)
+        def scale(m, n, engine, first, width):
+            cols = result_cols(m, n)[:, first : first + width].rearrange("q (p c) -> q p c", c=4)
+            engine.tensor_tensor(out=cols, in0=cols, in1=dinv_wide[n][:, first // 4 : (first + width) // 4, :], op=ALU.mult)
 
         def store(m, half):
             nc.sync.dma_start(out=out_rows[:, m, half * HALF : (half + 1) * HALF], in_=result[m, half][:])
@@ -204,7 +226,42 @@ def tile_reduced_basis_jacobi_residual_s1_kernel(
         def store_block(m, n):
             nc.sync.dma_start(out=out_rows[:, m, n * N_TILE : (n + 1) * N_TILE], in_=result_cols(m, n))
 
-        clear_tail_scales(0)
+        def prepare(items, tag):
+            bank = turn(items, tag)
+            grouped = new_grouped(len(items))
+            copy_turned(bank, grouped, 0)
+            return grouped
+
+        def prepare_row(m):
+            banks = [turn([(m, 0), (m, 1)], "turned_0"), turn([(m, 2), (m, LEAD)], "turned_1")]
+            grouped = new_grouped(PASSES)
+            copy_turned(banks[0], grouped, 0)
+            copy_turned(banks[1], grouped, 2)
+            return grouped
+
+        def spread_chunk(n, tag):
+            pairs = spread(n, tag)
+            copy_spread(n, pairs, 0, load_wide, "load_wide")
+            if n % 2 == 0:
+                copy_spread(n, pairs, 1, dinv_wide, "dinv_wide")
+            else:
+                dinv_wide[n] = pairs[:, 1]
+
+        def row_items(m):
+            return [(m, g) for g in range(PASSES)]
+
+        def finish(m, n):
+            if n % 2 == 0:
+                residual(m, n, acc[m, n][:], 0, N_TILE)
+                scale(m, n, nc.gpsimd, 0, N_TILE)
+            else:
+                for first in (0, 256):
+                    residual(m, n, acc[m, n][:, first : first + 256], first, 256)
+                for first in (0, 256):
+                    scale(m, n, nc.vector, first, 256)
+
+        clear_tail_scales(0, 2)
+        clear_tail_scales(2, 2)
         identity = keep.tile([P, P], F32)
         make_identity(nc, identity[:])
         load_in = keep.tile([P, CHUNKS, 4], BF16)
@@ -214,16 +271,16 @@ def tile_reduced_basis_jacobi_residual_s1_kernel(
         nc.scalar.dma_start(out=load_in[:], in_=load.rearrange("(h p c) -> p h c", h=CHUNKS, c=4))
         nc.scalar.dma_start(out=dinv_in[:], in_=dinv.rearrange("(h p c) -> p h c", h=CHUNKS, c=4))
         nc.gpsimd.dma_start(out=kappa_in[:], in_=kappa.rearrange("(p i) -> p i", i=ROWS))
-        load_tail_scales(0)
-        clear_tail_scales(1)
-        for g in range(TAIL_PASSES):
-            load_tail_words(0, [g])
+        load_tail_scales(0, 2)
+        load_tail_words(0, 2, [0])
+        load_tail_words(0, 2, [1])
         load_c_tail(1)
+        load_tail_words(0, 2, [2])
         load_c_lead(0)
         load_a_lead(0)
-        load_a_lead(1)
         load_c_tail(2)
         load_c_lead(2)
+        load_a_lead(1)
         load_c_tail(3)
         load_c_tail(4)
         load_c_lead(4)
@@ -233,112 +290,119 @@ def tile_reduced_basis_jacobi_residual_s1_kernel(
         load_c_tail(6)
         load_c_lead(6)
         load_c_tail(7)
-        load_tail_scales(1)
-        load_tail_words(1, list(range(TAIL_PASSES)))
+        load_tail_scales(2, 2)
+        load_tail_words(2, 2, [0, 1, 2])
 
         pairs_in = keep.tile([P, 4 * CHUNKS, 2], BF16)
         nc.vector.tensor_copy(out=pairs_in[:, :, 0], in_=load_in[:].rearrange("p h c -> p (h c)"))
         nc.vector.tensor_copy(out=pairs_in[:, :, 1], in_=dinv_in[:].rearrange("p h c -> p (h c)"))
         pair_words = pairs_in[:].rearrange("p a e -> p (a e)").bitcast(F32)
 
-        def prepare(items):
-            bank = turn(items)
-            grouped = new_grouped(len(items))
-            copy_turned(bank, grouped, 0)
-            return grouped
+        def passes(g, blocks):
+            for m, n in blocks:
+                multiply(m, n, g)
 
-        def prepare_row(m):
-            banks = [turn([(m, 0), (m, 1)]), turn([(m, 2), (m, LEAD)])]
-            grouped = new_grouped(PASSES)
-            copy_turned(banks[0], grouped, 0)
-            copy_turned(banks[1], grouped, 2)
-            return grouped
-
-        def spread_both(n, tag, bufs):
-            pairs = spread(n, tag, bufs)
-            copy_spread(n, pairs, 0, load_wide, "load_wide")
-            copy_spread(n, pairs, 1, dinv_wide, "dinv_wide")
-
-        def row_items(m):
-            return [(m, g) for g in range(PASSES)]
-
-        for items in ([(0, 0), (0, 1)], [(0, 2)]):
-            quantize_c(items, prepare(items))
-        spread_both(0, "acc", 5)
-        for g in (0, 1):
-            for n in (0, 1):
-                multiply(0, n, g)
-        for items in ([(1, 0), (1, 1)], [(1, 2)]):
-            quantize_c(items, prepare(items))
+        for key in ((0, "tail"), (1, "tail"), (0, "lead")):
+            take_stepped(key)
+        quantize_c([(0, 0), (0, 1)], prepare([(0, 0), (0, 1)], "turned_0"))
+        quantize_c([(0, 2)], prepare([(0, 2)], "turned_1"))
+        spread_chunk(0, "spare")
+        spread_chunk(1, "held")
+        passes(0, [(0, 0), (0, 1)])
+        passes(1, [(0, 0), (0, 1)])
+        quantize_c([(1, 0), (1, 1)], prepare([(1, 0), (1, 1)], "turned_0"))
+        quantize_c([(1, 2)], prepare([(1, 2)], "turned_1"))
+        passes(2, [(0, 0), (0, 1)])
         lead_items = [(0, LEAD), (1, LEAD)]
-        lead_grouped = prepare(lead_items)
-        spread_both(1, "acc", 5)
-        for n in (0, 1):
-            multiply(0, n, 2)
+        lead_grouped = prepare(lead_items, "spare")
         for g in range(TAIL_PASSES):
-            for n in (0, 1):
-                multiply(1, n, g)
+            passes(g, [(1, 0), (1, 1)])
+        sort_words((2, "tail"))
+        sort_words((2, "lead"))
         neg_kappa = keep.tile([P, ROWS], F32)
-        group_a_lead(0, nc.vector.tensor_copy)
+        nc.vector.tensor_scalar(out=neg_kappa[:], in0=kappa_in[:], scalar1=-1.0, scalar2=None, op0=ALU.mult)
+        group_a_lead(0, nc.vector.tensor_copy, 0, SPLIT)
         quantize_c(lead_items, lead_grouped)
         quantize_a_lead(0)
-        group_a_lead(1, nc.vector.tensor_copy)
-        nc.vector.tensor_scalar(out=neg_kappa[:], in0=kappa_in[:], scalar1=-1.0, scalar2=None, op0=ALU.mult)
+        quantize_c([(2, 0), (2, 1)], prepare([(2, 0), (2, 1)], "turned_0"))
+        quantize_c([(2, 2), (2, LEAD)], prepare([(2, 2), (2, LEAD)], "turned_1"))
+        passes(LEAD, [(0, 0), (1, 0)])
+        multiply_block(2, 0)
+        group_a_lead(1, nc.vector.tensor_copy, 0, 512)
+        sort_words((3, "tail"))
+        residual(0, 0, acc[0, 0][:], 0, N_TILE)
         quantize_a_lead(1)
-        quantize_c(row_items(2), prepare_row(2))
-        for n in (0, 1):
-            for m in (0, 1):
-                multiply(m, n, LEAD)
-        residual(0, 0)
-        residual(1, 0)
-        residual(0, 1)
+        residual(1, 0, acc[1, 0][:], 0, N_TILE)
+        grouped = prepare_row(3)
+        sort_words((4, "tail"))
+        sort_words((4, "lead"))
+        for g in range(TAIL_PASSES):
+            multiply(2, 1, g)
+        passes(LEAD, [(0, 1), (1, 1), (2, 1)])
+        quantize_c(row_items(3), grouped)
+        finish(2, 0)
+        finish(0, 1)
+        finish(1, 1)
 
-        for m in range(2, ROWS):
+        for m in range(3, ROWS):
             ahead = m + 1
             if ahead < ROWS:
                 grouped = prepare_row(ahead)
-            if ahead == ROWS - 2:
-                spread_both(2, "turned", 3)
-            if ahead == ROWS - 1:
-                pairs = spread(3, "turned", 3)
-                copy_spread(3, pairs, 0, load_wide, "load_wide")
-                dinv_wide[3] = pairs[:, 1]
-            if m in (3, 4):
-                group_a_lead(m - 1, nc.scalar.copy)
-            residual(m - 1, 1)
-            multiply_block(m, 0)
-            if m > 2:
-                scale(m - 2, 0, nc.vector)
-                scale(m - 2, 1, nc.vector)
-                store(m - 2, 0)
-            if ahead < ROWS:
+            if ahead + 1 < ROWS:
+                sort_words((ahead + 1, "tail"))
+                if ahead % 2 == 1:
+                    sort_words((ahead + 1, "lead"))
+            if ahead >= ROWS - 2 and ahead < ROWS:
+                spread_chunk(ahead - 4, "spare")
+            if m in (3, 6, 7):
+                group_a_lead(2 + m // 6, nc.scalar.copy, (m % 3) * 256, (m % 3 + 1) * 256)
+            if m == 3:
                 quantize_c(row_items(ahead), grouped)
-            residual(m, 0)
-            if m == 2:
-                scale(0, 0, nc.vector)
-                scale(0, 1, nc.vector)
-                store(0, 0)
-            if m in (4, 5):
-                quantize_a_lead(m - 2)
+            finish(m - 1, 1)
+            store(m - 1, 0)
+            multiply_block(m, 0)
+            if 3 < m < ROWS - 1:
+                quantize_c(row_items(ahead), grouped)
+            if m == 5:
+                group_a_lead(2, nc.vector.tensor_copy, 256, 512)
+            if m == 6:
+                quantize_a_lead(2)
+            finish(m, 0)
             multiply_block(m, 1)
         last = ROWS - 1
-        scale(last - 1, 0, nc.vector)
-        scale(last - 1, 1, nc.vector)
-        store(last - 1, 0)
-        residual(last, 1)
-        scale(last, 0, nc.vector)
-        scale(last, 1, nc.gpsimd)
+        quantize_a_lead(3)
+        finish(last, 1)
         store(last, 0)
 
         for m in range(ROWS):
-            multiply_block(m, 2)
-            residual(m, 2)
-            scale(m, 2, nc.gpsimd)
-            if m > 0:
-                scale(m - 1, 3, nc.vector)
-                store(m - 1, 1)
-            multiply_block(m, 3)
-            residual(m, 3)
+            for n in (2, 3):
+                if (m, n) != (last, 3):
+                    multiply_block(m, n)
+                    finish(m, n)
+                    if m < last:
+                        store_block(m, n)
+                    if n == 2 and m in (1, 3):
+                        scale(m // 2, 0, nc.gpsimd, 0, N_TILE)
+                        store(m // 2, 0)
+        quarter_tags = ["turned_0", "turned_1", "held", acc_tag(last, 3)]
+        for q in range(4):
+            bank = psum.tile([P, P], F32, name="quarter", tag=quarter_tags[q])
+            cols = slice(q * P, (q + 1) * P)
+            for g in range(PASSES):
+                nc.tensor.matmul_mx(
+                    out=bank[:],
+                    lhsT=c_mx[last, g][0],
+                    lhsT_scale=c_mx[last, g][1],
+                    rhs=a_mx[g, 3][0][:, cols],
+                    rhs_scale=a_mx[g, 3][1][:, cols],
+                    start=(g == 0),
+                    stop=(g == LEAD),
+                )
+            residual(last, 3, bank[:], q * P, P)
+            if q > 0:
+                scale(last, 3, nc.vector, (q - 1) * P, P)
+            if q == 2:
+                nc.sync.dma_start(out=out_rows[:, last, 3 * N_TILE : 3 * N_TILE + 2 * P], in_=result_cols(last, 3)[:, : 2 * P])
+        scale(last, 3, nc.vector, 3 * P, P)
+        nc.sync.dma_start(out=out_rows[:, last, 3 * N_TILE + 2 * P :], in_=result_cols(last, 3)[:, 2 * P :])
         store_block(last, 2)
-        scale(last, 3, nc.vector)
-        store_block(last, 3)

@@ -223,8 +223,9 @@ def tile_reduced_basis_jacobi_residual_s1_kernel(
         def store(m, half):
             nc.sync.dma_start(out=out_rows[:, m, half * HALF : (half + 1) * HALF], in_=result[m, half][:])
 
-        def store_block(m, n):
-            nc.sync.dma_start(out=out_rows[:, m, n * N_TILE : (n + 1) * N_TILE], in_=result_cols(m, n))
+        def store_cols(m, n, first, width):
+            start = n * N_TILE + first
+            nc.sync.dma_start(out=out_rows[:, m, start : start + width], in_=result_cols(m, n)[:, first : first + width])
 
         def prepare(items, tag):
             bank = turn(items, tag)
@@ -315,7 +316,7 @@ def tile_reduced_basis_jacobi_residual_s1_kernel(
         passes(2, [(0, 0), (0, 1)])
         lead_items = [(0, LEAD), (1, LEAD)]
         lead_grouped = prepare(lead_items, "spare")
-        for g in range(TAIL_PASSES):
+        for g in (0, 1):
             passes(g, [(1, 0), (1, 1)])
         sort_words((2, "tail"))
         sort_words((2, "lead"))
@@ -326,6 +327,7 @@ def tile_reduced_basis_jacobi_residual_s1_kernel(
         quantize_a_lead(0)
         quantize_c([(2, 0), (2, 1)], prepare([(2, 0), (2, 1)], "turned_0"))
         quantize_c([(2, 2), (2, LEAD)], prepare([(2, 2), (2, LEAD)], "turned_1"))
+        passes(2, [(1, 0), (1, 1)])
         passes(LEAD, [(0, 0), (1, 0)])
         multiply_block(2, 0)
         group_a_lead(1, nc.vector.tensor_copy, 0, 512)
@@ -374,35 +376,38 @@ def tile_reduced_basis_jacobi_residual_s1_kernel(
         finish(last, 1)
         store(last, 0)
 
-        for m in range(ROWS):
+        for m in range(last):
             for n in (2, 3):
-                if (m, n) != (last, 3):
-                    multiply_block(m, n)
-                    finish(m, n)
-                    if m < last:
-                        store_block(m, n)
-                    if n == 2 and m in (1, 3):
-                        scale(m // 2, 0, nc.gpsimd, 0, N_TILE)
-                        store(m // 2, 0)
-        quarter_tags = ["turned_0", "turned_1", "held", acc_tag(last, 3)]
-        for q in range(4):
-            bank = psum.tile([P, P], F32, name="quarter", tag=quarter_tags[q])
-            cols = slice(q * P, (q + 1) * P)
-            for g in range(PASSES):
-                nc.tensor.matmul_mx(
-                    out=bank[:],
-                    lhsT=c_mx[last, g][0],
-                    lhsT_scale=c_mx[last, g][1],
-                    rhs=a_mx[g, 3][0][:, cols],
-                    rhs_scale=a_mx[g, 3][1][:, cols],
-                    start=(g == 0),
-                    stop=(g == LEAD),
-                )
-            residual(last, 3, bank[:], q * P, P)
-            if q > 0:
-                scale(last, 3, nc.vector, (q - 1) * P, P)
-            if q == 2:
-                nc.sync.dma_start(out=out_rows[:, last, 3 * N_TILE : 3 * N_TILE + 2 * P], in_=result_cols(last, 3)[:, : 2 * P])
-        scale(last, 3, nc.vector, 3 * P, P)
-        nc.sync.dma_start(out=out_rows[:, last, 3 * N_TILE + 2 * P :], in_=result_cols(last, 3)[:, 2 * P :])
-        store_block(last, 2)
+                multiply_block(m, n)
+                finish(m, n)
+                store_cols(m, n, 0, N_TILE)
+                if n == 2 and m in (1, 3):
+                    scale(m // 2, 0, nc.gpsimd, 0, N_TILE)
+                    store(m // 2, 0)
+        multiply_block(last, 2)
+        residual(last, 2, acc[last, 2][:, : 2 * P], 0, 2 * P)
+        scale(last, 2, nc.gpsimd, 0, 2 * P)
+        store_cols(last, 2, 0, 2 * P)
+        residual(last, 2, acc[last, 2][:, 2 * P :], 2 * P, 2 * P)
+        for first, width, tag in [(0, 2 * P, "turned_0"), (2 * P, P, "turned_1"), (3 * P, P, "held")]:
+            bank = psum.tile([P, width], F32, name="piece", tag=tag)
+            for start in range(0, width, P):
+                cols = slice(first + start, first + start + P)
+                for g in range(PASSES):
+                    nc.tensor.matmul_mx(
+                        out=bank[:, start : start + P],
+                        lhsT=c_mx[last, g][0],
+                        lhsT_scale=c_mx[last, g][1],
+                        rhs=a_mx[g, 3][0][:, cols],
+                        rhs_scale=a_mx[g, 3][1][:, cols],
+                        start=(g == 0),
+                        stop=(g == LEAD),
+                    )
+            residual(last, 3, bank[:], first, width)
+            if first == 2 * P:
+                scale(last, 3, nc.vector, 0, 2 * P)
+                store_cols(last, 3, 0, 2 * P)
+        scale(last, 2, nc.vector, 2 * P, 2 * P)
+        store_cols(last, 2, 2 * P, 2 * P)
+        scale(last, 3, nc.vector, 2 * P, 2 * P)
+        store_cols(last, 3, 2 * P, 2 * P)

@@ -18,106 +18,107 @@ ALU = mybir.AluOpType
 P = 128
 PACK = 4
 K_PASS = P * PACK
-ROWS = M // P
-N_TILE = 512
-CHUNKS = N // N_TILE
-HALF = N // 2
+ROW_TILES = M // P
+LAST = ROW_TILES - 1
+CHUNK = 512
+HALF_CHUNK = CHUNK // 2
+CHUNKS = N // CHUNK
+SWEEP = 2 * CHUNK
 TAIL_PASSES = KT // K_PASS
 LEAD = TAIL_PASSES
 PASSES = TAIL_PASSES + 1
-SPLIT = 512
+SCALE_ROWS = 4
+ACC_BANKS = 4
+HEAD_TILES = 3
 
 
 def tile_reduced_basis_jacobi_residual_s1_kernel(
     tc, c_lead, c_tail, a_lead, a_tail_words, a_tail_scales, kappa, load, dinv, out
 ):
     nc = tc.nc
-    c_lead_rows = c_lead.rearrange("(p i) k -> p i k", i=ROWS)
-    c_tail_rows = c_tail.rearrange("(p i) k -> p i k", i=ROWS)
-    out_rows = out.rearrange("(p i) n -> p i n", i=ROWS)
-    a_lead_rows = a_lead.rearrange("(p j) n -> p j n", j=PACK)
-    tail_words = a_tail_words.rearrange("g p b -> p g b")
-    tail_scale_rows = a_tail_scales.rearrange("g (q r) n -> r q g n", r=4)
+    c_lead_rows = c_lead.rearrange("(p m) k -> p m k", m=ROW_TILES)
+    c_tail_rows = c_tail.rearrange("(p m) k -> p m k", m=ROW_TILES)
+    out_rows = out.rearrange("(p m) n -> p m n", m=ROW_TILES)
+    a_lead_rows = a_lead.rearrange("(p t) n -> p t n", t=PACK)
+    tail_code_rows = a_tail_words.rearrange("g p b -> p g b")
+    tail_scale_rows = a_tail_scales.rearrange("g (q r) n -> r q g n", r=SCALE_ROWS)
 
     with ExitStack() as ctx:
         keep = ctx.enter_context(tc.tile_pool(name="keep", bufs=1))
-        stage = ctx.enter_context(tc.tile_pool(name="stage", bufs=3))
+        stage = ctx.enter_context(tc.tile_pool(name="stage", bufs=4))
         psum = ctx.enter_context(tc.psum_pool(name="psum", bufs=1))
         ctx.enter_context(tc.manual_schedule())
 
-        c_raw = {}
+        c_loaded = {}
         c_words = {}
         c_mx = {}
         a_mx = {}
-        a_lead_raw = {}
+        a_lead_loaded = {}
         a_lead_grouped = {}
         tail_planes = {}
-        tail_scale = {}
         load_wide = {}
-        dinv_wide = {}
+        dinv_sbuf = {}
+        dinv_psum = {}
         acc = {}
         result = {}
+
 
         def load_c_tail(m):
             raw = keep.tile([P, KT], BF16, name="c_tail_%d" % m, align_bytes=64)
             nc.sync.dma_start(out=raw[:], in_=c_tail_rows[:, m, :])
-            c_raw[m, "tail"] = (raw[:].bitcast(F32), [(m, g) for g in range(TAIL_PASSES)])
+            c_loaded[m, "tail"] = (raw[:].bitcast(F32), [(m, g) for g in range(TAIL_PASSES)])
 
         def load_c_lead(m):
             raw = keep.tile([P, 2 * KL], BF16, name="c_lead_%d" % m, align_bytes=64)
+            nc.sync.dma_start(out=raw[:], in_=c_lead_rows[:, m : m + 2, :].rearrange("p m k -> p (m k)"))
+            c_loaded[m, "lead"] = (raw[:].bitcast(F32), [(m, LEAD), (m + 1, LEAD)])
+
+        def load_a_lead(n):
+            raw = keep.tile([P, PACK, CHUNK], BF16, name="a_lead_%d" % n, align_bytes=64)
+            nc.sync.dma_start(out=raw[:], in_=a_lead_rows[:, :, n * CHUNK : (n + 1) * CHUNK])
+            a_lead_loaded[n] = raw
+
+        def clear_tail_scales(sweep):
+            plane = keep.tile([P, TAIL_PASSES, SWEEP], U8, name="tail_scales_%d" % sweep, align_bytes=64)
+            nc.vector.memset(plane[:].rearrange("p g n -> p (g n)").bitcast(I32), 0)
+            tail_planes[sweep] = plane
+
+        def load_tail_scales(sweep):
+            for r in range(SCALE_ROWS):
+                nc.sync.dma_start(
+                    out=tail_planes[sweep][r:P:32, :, :].bitcast(I32),
+                    in_=tail_scale_rows[r][:, :, sweep * SWEEP : (sweep + 1) * SWEEP].bitcast(I32),
+                )
+
+        def load_tail_codes(sweep, first, count):
+            codes = keep.tile([P, count, 2 * SWEEP], U8, name="tail_codes_%d_%d" % (sweep, first), align_bytes=64)
             nc.sync.dma_start(
-                out=raw[:], in_=c_lead_rows[:, m : m + 2, :].rearrange("p i k -> p (i k)")
+                out=codes[:].bitcast(I32),
+                in_=tail_code_rows[:, first : first + count, 2 * sweep * SWEEP : 2 * (sweep + 1) * SWEEP].bitcast(I32),
             )
-            c_raw[m, "lead"] = (raw[:].bitcast(F32), [(m, LEAD), (m + 1, LEAD)])
+            for s in range(count):
+                for j in range(2):
+                    a_mx[first + s, 2 * sweep + j] = (
+                        codes[:, s, 2 * j * CHUNK : 2 * (j + 1) * CHUNK].bitcast(FP4X4),
+                        tail_planes[sweep][:, first + s, j * CHUNK : (j + 1) * CHUNK],
+                    )
+
 
         def take_stepped(key):
-            words, items = c_raw[key]
+            words, items = c_loaded[key]
             for s, item in enumerate(items):
                 c_words[item] = [words[:, 2 * P * s + u : 2 * P * (s + 1) : 2] for u in range(2)]
 
         def sort_words(key):
-            words, items = c_raw[key]
-            ordered = keep.tile([P, 2, len(items) * P], F32, name="c_sorted_" + key[1], tag="c_sorted_" + key[1], bufs=2)
+            words, items = c_loaded[key]
+            tag = "c_sorted_" + key[1]
+            ordered = keep.tile([P, 2, len(items) * P], F32, name=tag, tag=tag, bufs=3)
             nc.scalar.copy(
                 out=ordered[:].rearrange("p u (b i) -> p b u i", i=4),
                 in_=words.rearrange("p (b i u) -> p b u i", i=4, u=2),
             )
             for s, item in enumerate(items):
                 c_words[item] = [ordered[:, u, P * s : P * (s + 1)] for u in range(2)]
-
-        def load_a_lead(n):
-            raw = keep.tile([P, PACK, N_TILE], BF16, name="a_lead_%d" % n, align_bytes=64)
-            nc.sync.dma_start(out=raw[:], in_=a_lead_rows[:, :, n * N_TILE : (n + 1) * N_TILE])
-            a_lead_raw[n] = raw
-
-        def clear_tail_scales(first, count):
-            plane = keep.tile([P, TAIL_PASSES, count * N_TILE], U8, name="tail_scales_%d" % first, align_bytes=64)
-            nc.vector.memset(plane[:].rearrange("p g n -> p (g n)").bitcast(I32), 0)
-            tail_planes[first] = plane
-
-        def load_tail_scales(first, count):
-            cols = slice(first * N_TILE, (first + count) * N_TILE)
-            for r in range(4):
-                nc.sync.dma_start(
-                    out=tail_planes[first][r:P:32, :, :].bitcast(I32),
-                    in_=tail_scale_rows[r][:, :, cols].bitcast(I32),
-                )
-            for j in range(count):
-                for g in range(TAIL_PASSES):
-                    tail_scale[g, first + j] = tail_planes[first][:, g, j * N_TILE : (j + 1) * N_TILE]
-
-        def load_tail_words(first, count, passes):
-            codes = keep.tile(
-                [P, len(passes), 2 * count * N_TILE], U8, name="tail_words_%d_%d" % (first, passes[0]), align_bytes=64
-            )
-            cols = slice(2 * first * N_TILE, 2 * (first + count) * N_TILE)
-            nc.sync.dma_start(
-                out=codes[:].bitcast(I32), in_=tail_words[:, passes[0] : passes[-1] + 1, cols].bitcast(I32)
-            )
-            for s, g in enumerate(passes):
-                for j in range(count):
-                    words = codes[:, s, 2 * j * N_TILE : 2 * (j + 1) * N_TILE].bitcast(FP4X4)
-                    a_mx[g, first + j] = (words, tail_scale[g, first + j])
 
         def turn(items, tag):
             bank = psum.tile([P, 2 * len(items), P], F32, name="turned", tag=tag)
@@ -126,157 +127,151 @@ def tile_reduced_basis_jacobi_residual_s1_kernel(
                     nc.tensor.transpose(bank[:, 2 * s + u, :], c_words[item][u], identity[:])
             return bank
 
-        def new_grouped(count):
-            grouped = stage.tile([P, count * K_PASS], BF16, name="c_grouped", tag="c_grouped", align_bytes=64)
-            return grouped
-
-        def copy_turned(bank, grouped, first):
+        def copy_turned(bank):
             count = bank.shape[1] // 2
-            words = grouped[:, first * K_PASS : (first + count) * K_PASS].bitcast(F32)
+            grouped = stage.tile([P, count * K_PASS], BF16, name="c_grouped", tag="c_grouped", align_bytes=64)
             nc.scalar.copy(
-                out=words.rearrange("p (s r u) -> p s r u", s=count, u=2),
+                out=grouped[:].bitcast(F32).rearrange("p (s r u) -> p s r u", s=count, u=2),
                 in_=bank[:].rearrange("p (s u) r -> p s r u", u=2),
             )
+            return grouped
 
         def quantize_c(items, grouped):
             name = "%d_%d" % items[0]
             codes = keep.tile([P, len(items) * P], U32, name="c_codes_" + name, align_bytes=64)
-            scales = keep.tile([P, len(items) * P], U8, name="c_scales_" + name, align_bytes=64)
-            nc.vector.quantize_mx(out=codes[:].bitcast(FP8X4), scales=scales[:], in_=grouped[:])
+            plane = keep.tile([P, len(items) * P], U8, name="c_scales_" + name, align_bytes=64)
+            nc.vector.quantize_mx(out=codes[:].bitcast(FP8X4), scales=plane[:], in_=grouped[:])
             for s, item in enumerate(items):
                 cols = slice(s * P, (s + 1) * P)
-                c_mx[item] = (codes[:, cols].bitcast(FP8X4), scales[:, cols])
+                c_mx[item] = (codes[:, cols].bitcast(FP8X4), plane[:, cols])
 
-        def group_a_lead(n, copy, first=0, last=N_TILE):
+        def prepare_items(items, tag):
+            quantize_c(items, copy_turned(turn(items, tag)))
+
+        def turn_row_tile(m):
+            banks = [turn([(m, 0), (m, 1)], "turned_0"), turn([(m, 2), (m, LEAD)], "turned_1")]
+            return [copy_turned(bank) for bank in banks]
+
+        def quantize_row_tile(m, grouped):
+            quantize_c([(m, 0), (m, 1)], grouped[0])
+            quantize_c([(m, 2), (m, LEAD)], grouped[1])
+
+
+        def group_a_lead(n, copy, first, width):
             if n not in a_lead_grouped:
-                a_lead_grouped[n] = keep.tile([P, N_TILE, PACK], BF16, name="a_grouped_%d" % n, align_bytes=64)
+                a_lead_grouped[n] = keep.tile([P, CHUNK, PACK], BF16, name="a_grouped_%d" % n, align_bytes=64)
             copy(
-                out=a_lead_grouped[n][:, first:last, :].rearrange("p (c i) t -> p c t i", i=4),
-                in_=a_lead_raw[n][:, :, first:last].rearrange("p t (c i) -> p c t i", i=4),
+                out=a_lead_grouped[n][:, first : first + width, :].rearrange("p (c i) t -> p c t i", i=4),
+                in_=a_lead_loaded[n][:, :, first : first + width].rearrange("p t (c i) -> p c t i", i=4),
             )
 
         def quantize_a_lead(n):
-            codes = keep.tile([P, N_TILE], U32, name="a_codes_%d" % n, align_bytes=64)
-            scales = keep.tile([P, N_TILE], U8, name="a_scales_%d" % n, align_bytes=64)
+            codes = keep.tile([P, CHUNK], U32, name="a_codes_%d" % n, align_bytes=64)
+            plane = keep.tile([P, CHUNK], U8, name="a_scales_%d" % n, align_bytes=64)
             nc.vector.quantize_mx(
-                out=codes[:].bitcast(FP8X4),
-                scales=scales[:],
-                in_=a_lead_grouped[n][:].rearrange("p c t -> p (c t)"),
+                out=codes[:].bitcast(FP8X4), scales=plane[:], in_=a_lead_grouped[n][:].rearrange("p c t -> p (c t)")
             )
-            a_mx[LEAD, n] = (codes[:].bitcast(FP8X4), scales[:])
+            a_mx[LEAD, n] = (codes[:].bitcast(FP8X4), plane[:])
 
-        def spread(n, tag):
+
+        def copy_wide(values, name):
+            wide = keep.tile([P, CHUNK], F32, name=name)
+            nc.scalar.copy(out=wide[:].rearrange("q (p c) -> q p c", c=4), in_=values)
+            return wide
+
+        def spread_chunk(n, tag):
             bank = psum.tile([P, 4, P], F32, name="spread", tag=tag)
             for c in range(4):
                 column = pair_words[:, 4 * n + c : 4 * n + c + 1].to_broadcast([P, P])
                 nc.tensor.transpose(bank[:, c, :], column, identity[:])
-            return bank[:].rearrange("q c p -> q (c p)").bitcast(BF16).rearrange("q (c p e) -> q e p c", c=4, e=2)
+            pairs = bank[:].rearrange("q c p -> q (c p)").bitcast(BF16).rearrange("q (c p e) -> q e p c", c=4, e=2)
+            load_wide[n] = copy_wide(pairs[:, 0], "load_wide_%d" % n)
+            if n % 2 == 1:
+                dinv_psum[n] = pairs[:, 1]
+            if n < CHUNKS - 1:
+                dinv_sbuf[n] = copy_wide(pairs[:, 1], "dinv_wide_%d" % n)[:].rearrange("q (p c) -> q p c", c=4)
 
-        def copy_spread(n, pairs, which, table, name):
-            wide = keep.tile([P, N_TILE], F32, name="%s_%d" % (name, n))
-            nc.scalar.copy(out=wide[:].rearrange("q (p c) -> q p c", c=4), in_=pairs[:, which])
-            table[n] = wide[:].rearrange("q (p c) -> q p c", c=4)
 
         def acc_tag(m, n):
             if (m, n) == (2, 0):
                 return "spare"
-            order = m + 2 * n if m < 2 and n < 2 else 2 * m + n % 2 - 1 + (2 * ROWS if n > 1 else 0)
-            return "acc_%d" % (order % 4)
+            order = m + 2 * n if m < 2 and n < 2 else 2 * m + n % 2 - 1
+            return "acc_%d" % (order % ACC_BANKS)
 
-        def multiply(m, n, g):
-            if g == 0:
-                acc[m, n] = psum.tile([P, N_TILE], F32, name="acc", tag=acc_tag(m, n))
+        def multiply_cols(bank, m, n, g, first, width):
             nc.tensor.matmul_mx(
-                out=acc[m, n][:],
+                out=bank,
                 lhsT=c_mx[m, g][0],
                 lhsT_scale=c_mx[m, g][1],
-                rhs=a_mx[g, n][0],
-                rhs_scale=a_mx[g, n][1],
+                rhs=a_mx[g, n][0][:, first : first + width],
+                rhs_scale=a_mx[g, n][1][:, first : first + width],
                 start=(g == 0),
                 stop=(g == LEAD),
             )
 
+        def multiply(g, blocks):
+            for m, n in blocks:
+                if g == 0:
+                    acc[m, n] = psum.tile([P, CHUNK], F32, name="acc", tag=acc_tag(m, n))
+                multiply_cols(acc[m, n][:], m, n, g, 0, CHUNK)
+
         def multiply_block(m, n):
             for g in range(PASSES):
-                multiply(m, n, g)
+                multiply(g, [(m, n)])
 
-        def result_cols(m, n):
-            half, j = divmod(n, 2)
-            if (m, half) not in result:
-                result[m, half] = keep.tile([P, HALF], F32, name="result_%d_%d" % (m, half))
-            return result[m, half][:, j * N_TILE : (j + 1) * N_TILE]
 
-        def residual(m, n, bank, first, width):
+        def result_cols(m, n, first, width):
+            sweep, j = divmod(n, 2)
+            if (m, sweep) not in result:
+                result[m, sweep] = keep.tile([P, SWEEP], F32, name="result_%d_%d" % (m, sweep))
+            return result[m, sweep][:, j * CHUNK + first : j * CHUNK + first + width]
+
+        def residual_from(bank, m, n, first, width):
             nc.vector.scalar_tensor_tensor(
-                out=result_cols(m, n)[:, first : first + width],
+                out=result_cols(m, n, first, width),
                 in0=bank,
                 scalar=neg_kappa[:, m : m + 1],
-                in1=load_wide[n].rearrange("q p c -> q (p c)")[:, first : first + width],
+                in1=load_wide[n][:, first : first + width],
                 op0=ALU.mult,
                 op1=ALU.add,
             )
 
-        def scale(m, n, engine, first, width):
-            cols = result_cols(m, n)[:, first : first + width].rearrange("q (p c) -> q p c", c=4)
-            engine.tensor_tensor(out=cols, in0=cols, in1=dinv_wide[n][:, first // 4 : (first + width) // 4, :], op=ALU.mult)
+        def residual(m, n, first=0, width=CHUNK):
+            residual_from(acc[m, n][:, first : first + width], m, n, first, width)
 
-        def store(m, half):
-            nc.sync.dma_start(out=out_rows[:, m, half * HALF : (half + 1) * HALF], in_=result[m, half][:])
+        def scale(engine, table, m, n, first, width):
+            cols = result_cols(m, n, first, width).rearrange("q (p c) -> q p c", c=4)
+            engine.tensor_tensor(out=cols, in0=cols, in1=table[n][:, first // 4 : (first + width) // 4, :], op=ALU.mult)
 
-        def store_cols(m, n, first, width):
-            start = n * N_TILE + first
-            nc.sync.dma_start(out=out_rows[:, m, start : start + width], in_=result_cols(m, n)[:, first : first + width])
+        def scale_on_vector(m, n, first=0, width=CHUNK):
+            scale(nc.vector, dinv_psum, m, n, first, width)
 
-        def prepare(items, tag):
-            bank = turn(items, tag)
-            grouped = new_grouped(len(items))
-            copy_turned(bank, grouped, 0)
-            return grouped
+        def scale_on_gpsimd(m, n, first=0, width=CHUNK):
+            scale(nc.gpsimd, dinv_sbuf, m, n, first, width)
 
-        def prepare_row(m):
-            banks = [turn([(m, 0), (m, 1)], "turned_0"), turn([(m, 2), (m, LEAD)], "turned_1")]
-            grouped = new_grouped(PASSES)
-            copy_turned(banks[0], grouped, 0)
-            copy_turned(banks[1], grouped, 2)
-            return grouped
+        def store_first_sweep(m):
+            nc.sync.dma_start(out=out_rows[:, m, :SWEEP], in_=result[m, 0][:])
 
-        def spread_chunk(n, tag):
-            pairs = spread(n, tag)
-            copy_spread(n, pairs, 0, load_wide, "load_wide")
-            if n % 2 == 0:
-                copy_spread(n, pairs, 1, dinv_wide, "dinv_wide")
-            else:
-                dinv_wide[n] = pairs[:, 1]
+        def store(m, n, first=0, width=CHUNK):
+            start = n * CHUNK + first
+            nc.sync.dma_start(out=out_rows[:, m, start : start + width], in_=result_cols(m, n, first, width))
 
-        def row_items(m):
-            return [(m, g) for g in range(PASSES)]
-
-        def finish(m, n):
-            if n % 2 == 0:
-                residual(m, n, acc[m, n][:], 0, N_TILE)
-                scale(m, n, nc.gpsimd, 0, N_TILE)
-            else:
-                for first in (0, 256):
-                    residual(m, n, acc[m, n][:, first : first + 256], first, 256)
-                for first in (0, 256):
-                    scale(m, n, nc.vector, first, 256)
-
-        clear_tail_scales(0, 2)
-        clear_tail_scales(2, 2)
+        clear_tail_scales(0)
+        clear_tail_scales(1)
         identity = keep.tile([P, P], F32)
         make_identity(nc, identity[:])
         load_in = keep.tile([P, CHUNKS, 4], BF16)
         dinv_in = keep.tile([P, CHUNKS, 4], BF16)
-        kappa_in = keep.tile([P, ROWS], BF16)
+        kappa_in = keep.tile([P, ROW_TILES], BF16)
         load_c_tail(0)
-        nc.scalar.dma_start(out=load_in[:], in_=load.rearrange("(h p c) -> p h c", h=CHUNKS, c=4))
-        nc.scalar.dma_start(out=dinv_in[:], in_=dinv.rearrange("(h p c) -> p h c", h=CHUNKS, c=4))
-        nc.gpsimd.dma_start(out=kappa_in[:], in_=kappa.rearrange("(p i) -> p i", i=ROWS))
-        load_tail_scales(0, 2)
-        load_tail_words(0, 2, [0])
-        load_tail_words(0, 2, [1])
+        nc.scalar.dma_start(out=load_in[:], in_=load.rearrange("(n p c) -> p n c", n=CHUNKS, c=4))
+        nc.scalar.dma_start(out=dinv_in[:], in_=dinv.rearrange("(n p c) -> p n c", n=CHUNKS, c=4))
+        nc.gpsimd.dma_start(out=kappa_in[:], in_=kappa.rearrange("(p m) -> p m", m=ROW_TILES))
+        load_tail_scales(0)
+        load_tail_codes(0, 0, 1)
+        load_tail_codes(0, 1, 1)
         load_c_tail(1)
-        load_tail_words(0, 2, [2])
+        load_tail_codes(0, 2, 1)
         load_c_lead(0)
         load_a_lead(0)
         load_c_tail(2)
@@ -291,123 +286,134 @@ def tile_reduced_basis_jacobi_residual_s1_kernel(
         load_c_tail(6)
         load_c_lead(6)
         load_c_tail(7)
-        load_tail_scales(2, 2)
-        load_tail_words(2, 2, [0, 1, 2])
+        load_tail_scales(1)
+        load_tail_codes(1, 0, TAIL_PASSES)
 
         pairs_in = keep.tile([P, 4 * CHUNKS, 2], BF16)
-        nc.vector.tensor_copy(out=pairs_in[:, :, 0], in_=load_in[:].rearrange("p h c -> p (h c)"))
-        nc.vector.tensor_copy(out=pairs_in[:, :, 1], in_=dinv_in[:].rearrange("p h c -> p (h c)"))
+        nc.vector.tensor_copy(out=pairs_in[:, :, 0], in_=load_in[:].rearrange("p n c -> p (n c)"))
+        nc.vector.tensor_copy(out=pairs_in[:, :, 1], in_=dinv_in[:].rearrange("p n c -> p (n c)"))
         pair_words = pairs_in[:].rearrange("p a e -> p (a e)").bitcast(F32)
-
-        def passes(g, blocks):
-            for m, n in blocks:
-                multiply(m, n, g)
 
         for key in ((0, "tail"), (1, "tail"), (0, "lead")):
             take_stepped(key)
-        quantize_c([(0, 0), (0, 1)], prepare([(0, 0), (0, 1)], "turned_0"))
-        quantize_c([(0, 2)], prepare([(0, 2)], "turned_1"))
+        prepare_items([(0, 0)], "turned_0")
+        prepare_items([(0, 1), (0, 2)], "turned_1")
         spread_chunk(0, "spare")
         spread_chunk(1, "held")
-        passes(0, [(0, 0), (0, 1)])
-        passes(1, [(0, 0), (0, 1)])
-        quantize_c([(1, 0), (1, 1)], prepare([(1, 0), (1, 1)], "turned_0"))
-        quantize_c([(1, 2)], prepare([(1, 2)], "turned_1"))
-        passes(2, [(0, 0), (0, 1)])
+        multiply(0, [(0, 0), (0, 1)])
+        multiply(1, [(0, 0), (0, 1)])
+        prepare_items([(1, 0), (1, 1)], "turned_0")
+        prepare_items([(1, 2)], "turned_1")
+        multiply(2, [(0, 0), (0, 1)])
         lead_items = [(0, LEAD), (1, LEAD)]
-        lead_grouped = prepare(lead_items, "spare")
-        for g in (0, 1):
-            passes(g, [(1, 0), (1, 1)])
+        lead_bank = turn(lead_items, "spare")
+        multiply(0, [(1, 0), (1, 1)])
+        multiply(1, [(1, 0), (1, 1)])
         sort_words((2, "tail"))
         sort_words((2, "lead"))
-        neg_kappa = keep.tile([P, ROWS], F32)
+        lead_grouped = copy_turned(lead_bank)
+        group_a_lead(0, nc.vector.tensor_copy, 0, CHUNK)
+        neg_kappa = keep.tile([P, ROW_TILES], F32)
         nc.vector.tensor_scalar(out=neg_kappa[:], in0=kappa_in[:], scalar1=-1.0, scalar2=None, op0=ALU.mult)
-        group_a_lead(0, nc.vector.tensor_copy, 0, SPLIT)
-        quantize_c(lead_items, lead_grouped)
         quantize_a_lead(0)
-        quantize_c([(2, 0), (2, 1)], prepare([(2, 0), (2, 1)], "turned_0"))
-        quantize_c([(2, 2), (2, LEAD)], prepare([(2, 2), (2, LEAD)], "turned_1"))
-        passes(2, [(1, 0), (1, 1)])
-        passes(LEAD, [(0, 0), (1, 0)])
+        quantize_c(lead_items, lead_grouped)
+        group_a_lead(1, nc.vector.tensor_copy, 0, HALF_CHUNK)
+        prepare_items([(2, 0), (2, 1)], "turned_0")
+        prepare_items([(2, 2), (2, LEAD)], "turned_1")
+        multiply(2, [(1, 0), (1, 1)])
+        multiply(LEAD, [(0, 0), (1, 0)])
         multiply_block(2, 0)
-        group_a_lead(1, nc.vector.tensor_copy, 0, 512)
-        sort_words((3, "tail"))
-        residual(0, 0, acc[0, 0][:], 0, N_TILE)
+        group_a_lead(1, nc.vector.tensor_copy, HALF_CHUNK, HALF_CHUNK)
+        residual(0, 0)
         quantize_a_lead(1)
-        residual(1, 0, acc[1, 0][:], 0, N_TILE)
-        grouped = prepare_row(3)
+        residual(1, 0)
+        sort_words((3, "tail"))
         sort_words((4, "tail"))
         sort_words((4, "lead"))
+        grouped = turn_row_tile(3)
+        sort_words((5, "tail"))
         for g in range(TAIL_PASSES):
-            multiply(2, 1, g)
-        passes(LEAD, [(0, 1), (1, 1), (2, 1)])
-        quantize_c(row_items(3), grouped)
-        finish(2, 0)
-        finish(0, 1)
-        finish(1, 1)
+            multiply(g, [(2, 1)])
+        multiply(LEAD, [(0, 1), (1, 1), (2, 1)])
+        quantize_row_tile(3, grouped)
+        residual(2, 0)
+        scale_on_gpsimd(2, 0)
+        residual(0, 1)
+        residual(1, 1)
 
-        for m in range(3, ROWS):
-            ahead = m + 1
-            if ahead < ROWS:
-                grouped = prepare_row(ahead)
-            if ahead + 1 < ROWS:
-                sort_words((ahead + 1, "tail"))
-                if ahead % 2 == 1:
-                    sort_words((ahead + 1, "lead"))
-            if ahead >= ROWS - 2 and ahead < ROWS:
-                spread_chunk(ahead - 4, "spare")
-            if m in (3, 6, 7):
-                group_a_lead(2 + m // 6, nc.scalar.copy, (m % 3) * 256, (m % 3 + 1) * 256)
-            if m == 3:
-                quantize_c(row_items(ahead), grouped)
-            finish(m - 1, 1)
-            store(m - 1, 0)
+        for m in range(HEAD_TILES, ROW_TILES):
+            if m + 1 <= LAST:
+                grouped = turn_row_tile(m + 1)
+            if m + 3 <= LAST:
+                sort_words((m + 3, "tail"))
+                if (m + 3) % 2 == 0:
+                    sort_words((m + 3, "lead"))
+            if m + 1 in (LAST - 1, LAST):
+                spread_chunk(m + 1 - LAST + 3, "spare")
+            n, half = divmod(m, 2)
+            if m > HEAD_TILES and m + 1 != LAST - 1:
+                group_a_lead(n, nc.scalar.copy, half * HALF_CHUNK, HALF_CHUNK)
+            residual(m - 1, 1)
             multiply_block(m, 0)
-            if 3 < m < ROWS - 1:
-                quantize_c(row_items(ahead), grouped)
-            if m == 5:
-                group_a_lead(2, nc.vector.tensor_copy, 256, 512)
-            if m == 6:
-                quantize_a_lead(2)
-            finish(m, 0)
+            if m + 1 <= LAST:
+                quantize_row_tile(m + 1, grouped)
+            if m + 1 == LAST - 1:
+                group_a_lead(n, nc.vector.tensor_copy, half * HALF_CHUNK, HALF_CHUNK)
+            if m >= LAST - 1:
+                quantize_a_lead(m - LAST + 3)
+            residual(m, 0)
+            scale_on_gpsimd(m, 0)
+            scale_on_vector(m - 1, 1)
+            store_first_sweep(m - 1)
             multiply_block(m, 1)
-        last = ROWS - 1
-        quantize_a_lead(3)
-        finish(last, 1)
-        store(last, 0)
 
-        for m in range(last):
-            for n in (2, 3):
-                multiply_block(m, n)
-                finish(m, n)
-                store_cols(m, n, 0, N_TILE)
-                if n == 2 and m in (1, 3):
-                    scale(m // 2, 0, nc.gpsimd, 0, N_TILE)
-                    store(m // 2, 0)
-        multiply_block(last, 2)
-        residual(last, 2, acc[last, 2][:, : 2 * P], 0, 2 * P)
-        scale(last, 2, nc.gpsimd, 0, 2 * P)
-        store_cols(last, 2, 0, 2 * P)
-        residual(last, 2, acc[last, 2][:, 2 * P :], 2 * P, 2 * P)
-        for first, width, tag in [(0, 2 * P, "turned_0"), (2 * P, P, "turned_1"), (3 * P, P, "held")]:
+        late_blocks = [(m, n) for m in range(2) for n in range(2)]
+
+        def finish_late(s):
+            scale_on_gpsimd(*late_blocks[s])
+            store(*late_blocks[s])
+
+        finish_late(0)
+        residual(LAST, 1)
+
+        for m in range(LAST):
+            multiply_block(m, 2)
+            residual(m, 2)
+            scale_on_gpsimd(m, 2)
+            if m == 0:
+                scale_on_vector(LAST, 1)
+                store_first_sweep(LAST)
+            else:
+                scale_on_vector(m - 1, 3)
+                store(m - 1, 3)
+            store(m, 2)
+            if m + 1 < len(late_blocks):
+                finish_late(m + 1)
+            multiply_block(m, 3)
+            if m < LAST - 1:
+                residual(m, 3)
+
+        halves = (0, HALF_CHUNK)
+        for first in halves:
+            residual(LAST - 1, 3, first, HALF_CHUNK)
+        for first in halves:
+            scale_on_vector(LAST - 1, 3, first, HALF_CHUNK)
+        store(LAST - 1, 3)
+        multiply_block(LAST, 2)
+        for first in halves:
+            residual(LAST, 2, first, HALF_CHUNK)
+            scale_on_gpsimd(LAST, 2, first, HALF_CHUNK)
+        store(LAST, 2, 0, HALF_CHUNK)
+        for first, width, tag in ((0, 2 * P, "turned_0"), (2 * P, P, "turned_1"), (3 * P, P, "held")):
             bank = psum.tile([P, width], F32, name="piece", tag=tag)
             for start in range(0, width, P):
-                cols = slice(first + start, first + start + P)
                 for g in range(PASSES):
-                    nc.tensor.matmul_mx(
-                        out=bank[:, start : start + P],
-                        lhsT=c_mx[last, g][0],
-                        lhsT_scale=c_mx[last, g][1],
-                        rhs=a_mx[g, 3][0][:, cols],
-                        rhs_scale=a_mx[g, 3][1][:, cols],
-                        start=(g == 0),
-                        stop=(g == LEAD),
-                    )
-            residual(last, 3, bank[:], first, width)
-            if first == 2 * P:
-                scale(last, 3, nc.vector, 0, 2 * P)
-                store_cols(last, 3, 0, 2 * P)
-        scale(last, 2, nc.vector, 2 * P, 2 * P)
-        store_cols(last, 2, 2 * P, 2 * P)
-        scale(last, 3, nc.vector, 2 * P, 2 * P)
-        store_cols(last, 3, 2 * P, 2 * P)
+                    multiply_cols(bank[:, start : start + P], LAST, 3, g, first + start, P)
+            residual_from(bank[:], LAST, 3, first, width)
+            if first == HALF_CHUNK:
+                scale_on_vector(LAST, 3, 0, HALF_CHUNK)
+                store(LAST, 3, 0, HALF_CHUNK)
+        store(LAST, 2, HALF_CHUNK, HALF_CHUNK)
+        for first in (2 * P, 3 * P):
+            scale_on_vector(LAST, 3, first, P)
+        store(LAST, 3, HALF_CHUNK, HALF_CHUNK)

from contextlib import ExitStack

import concourse.mybir as mybir
from concourse.masks import make_identity

M, KL, KT, N = 1024, 512, 1536, 2048
FLOPS = 2 * M * (KL + KT) * N

F32 = mybir.dt.float32
BF16 = mybir.dt.bfloat16
I32 = mybir.dt.int32
U32 = mybir.dt.uint32
U8 = mybir.dt.uint8
FP8X4 = mybir.dt.float8_e4m3fn_x4
FP4X4 = mybir.dt.float4_e2m1fn_x4
ALU = mybir.AluOpType

P = 128
PACK = 4
K_PASS = P * PACK
ROW_TILES = M // P
LAST = ROW_TILES - 1
CHUNK = 512
HALF_CHUNK = CHUNK // 2
CHUNKS = N // CHUNK
SWEEP = 2 * CHUNK
TAIL_PASSES = KT // K_PASS
LEAD = TAIL_PASSES
PASSES = TAIL_PASSES + 1
SCALE_ROWS = 4
ACC_BANKS = 4
HEAD_TILES = 3


def tile_reduced_basis_jacobi_residual_s1_kernel(
    tc, c_lead, c_tail, a_lead, a_tail_words, a_tail_scales, kappa, load, dinv, out
):
    nc = tc.nc
    c_lead_rows = c_lead.rearrange("(p m) k -> p m k", m=ROW_TILES)
    c_tail_rows = c_tail.rearrange("(p m) k -> p m k", m=ROW_TILES)
    out_rows = out.rearrange("(p m) n -> p m n", m=ROW_TILES)
    a_lead_rows = a_lead.rearrange("(p t) n -> p t n", t=PACK)
    tail_code_rows = a_tail_words.rearrange("g p b -> p g b")
    tail_scale_rows = a_tail_scales.rearrange("g (q r) n -> r q g n", r=SCALE_ROWS)

    with ExitStack() as ctx:
        keep = ctx.enter_context(tc.tile_pool(name="keep", bufs=1))
        stage = ctx.enter_context(tc.tile_pool(name="stage", bufs=4))
        psum = ctx.enter_context(tc.psum_pool(name="psum", bufs=1))
        ctx.enter_context(tc.manual_schedule())

        c_loaded = {}
        c_words = {}
        c_mx = {}
        a_mx = {}
        a_lead_loaded = {}
        a_lead_grouped = {}
        tail_planes = {}
        load_wide = {}
        dinv_sbuf = {}
        dinv_psum = {}
        acc = {}
        result = {}


        def load_c_tail(m):
            raw = keep.tile([P, KT], BF16, name="c_tail_%d" % m, align_bytes=64)
            nc.sync.dma_start(out=raw[:], in_=c_tail_rows[:, m, :])
            c_loaded[m, "tail"] = (raw[:].bitcast(F32), [(m, g) for g in range(TAIL_PASSES)])

        def load_c_lead(m):
            raw = keep.tile([P, 2 * KL], BF16, name="c_lead_%d" % m, align_bytes=64)
            nc.sync.dma_start(out=raw[:], in_=c_lead_rows[:, m : m + 2, :].rearrange("p m k -> p (m k)"))
            c_loaded[m, "lead"] = (raw[:].bitcast(F32), [(m, LEAD), (m + 1, LEAD)])

        def load_a_lead(n):
            raw = keep.tile([P, PACK, CHUNK], BF16, name="a_lead_%d" % n, align_bytes=64)
            nc.sync.dma_start(out=raw[:], in_=a_lead_rows[:, :, n * CHUNK : (n + 1) * CHUNK])
            a_lead_loaded[n] = raw

        def clear_tail_scales(sweep):
            plane = keep.tile([P, TAIL_PASSES, SWEEP], U8, name="tail_scales_%d" % sweep, align_bytes=64)
            nc.vector.memset(plane[:].rearrange("p g n -> p (g n)").bitcast(I32), 0)
            tail_planes[sweep] = plane

        def load_tail_scales(sweep):
            for r in range(SCALE_ROWS):
                nc.sync.dma_start(
                    out=tail_planes[sweep][r:P:32, :, :].bitcast(I32),
                    in_=tail_scale_rows[r][:, :, sweep * SWEEP : (sweep + 1) * SWEEP].bitcast(I32),
                )

        def load_tail_codes(sweep, first, count):
            codes = keep.tile([P, count, 2 * SWEEP], U8, name="tail_codes_%d_%d" % (sweep, first), align_bytes=64)
            nc.sync.dma_start(
                out=codes[:].bitcast(I32),
                in_=tail_code_rows[:, first : first + count, 2 * sweep * SWEEP : 2 * (sweep + 1) * SWEEP].bitcast(I32),
            )
            for s in range(count):
                for j in range(2):
                    a_mx[first + s, 2 * sweep + j] = (
                        codes[:, s, 2 * j * CHUNK : 2 * (j + 1) * CHUNK].bitcast(FP4X4),
                        tail_planes[sweep][:, first + s, j * CHUNK : (j + 1) * CHUNK],
                    )


        def take_stepped(key):
            words, items = c_loaded[key]
            for s, item in enumerate(items):
                c_words[item] = [words[:, 2 * P * s + u : 2 * P * (s + 1) : 2] for u in range(2)]

        def sort_words(key):
            words, items = c_loaded[key]
            tag = "c_sorted_" + key[1]
            ordered = keep.tile([P, 2, len(items) * P], F32, name=tag, tag=tag, bufs=3)
            nc.scalar.copy(
                out=ordered[:].rearrange("p u (b i) -> p b u i", i=4),
                in_=words.rearrange("p (b i u) -> p b u i", i=4, u=2),
            )
            for s, item in enumerate(items):
                c_words[item] = [ordered[:, u, P * s : P * (s + 1)] for u in range(2)]

        def turn(items, tag):
            bank = psum.tile([P, 2 * len(items), P], F32, name="turned", tag=tag)
            for s, item in enumerate(items):
                for u in range(2):
                    nc.tensor.transpose(bank[:, 2 * s + u, :], c_words[item][u], identity[:])
            return bank

        def copy_turned(bank):
            count = bank.shape[1] // 2
            grouped = stage.tile([P, count * K_PASS], BF16, name="c_grouped", tag="c_grouped", align_bytes=64)
            nc.scalar.copy(
                out=grouped[:].bitcast(F32).rearrange("p (s r u) -> p s r u", s=count, u=2),
                in_=bank[:].rearrange("p (s u) r -> p s r u", u=2),
            )
            return grouped

        def quantize_c(items, grouped):
            name = "%d_%d" % items[0]
            codes = keep.tile([P, len(items) * P], U32, name="c_codes_" + name, align_bytes=64)
            plane = keep.tile([P, len(items) * P], U8, name="c_scales_" + name, align_bytes=64)
            nc.vector.quantize_mx(out=codes[:].bitcast(FP8X4), scales=plane[:], in_=grouped[:])
            for s, item in enumerate(items):
                cols = slice(s * P, (s + 1) * P)
                c_mx[item] = (codes[:, cols].bitcast(FP8X4), plane[:, cols])

        def prepare_items(items, tag):
            quantize_c(items, copy_turned(turn(items, tag)))

        def turn_row_tile(m):
            banks = [turn([(m, 0), (m, 1)], "turned_0"), turn([(m, 2), (m, LEAD)], "turned_1")]
            return [copy_turned(bank) for bank in banks]

        def quantize_row_tile(m, grouped):
            quantize_c([(m, 0), (m, 1)], grouped[0])
            quantize_c([(m, 2), (m, LEAD)], grouped[1])


        def group_a_lead(n, copy, first, width):
            if n not in a_lead_grouped:
                a_lead_grouped[n] = keep.tile([P, CHUNK, PACK], BF16, name="a_grouped_%d" % n, align_bytes=64)
            copy(
                out=a_lead_grouped[n][:, first : first + width, :].rearrange("p (c i) t -> p c t i", i=4),
                in_=a_lead_loaded[n][:, :, first : first + width].rearrange("p t (c i) -> p c t i", i=4),
            )

        def quantize_a_lead(n):
            codes = keep.tile([P, CHUNK], U32, name="a_codes_%d" % n, align_bytes=64)
            plane = keep.tile([P, CHUNK], U8, name="a_scales_%d" % n, align_bytes=64)
            nc.vector.quantize_mx(
                out=codes[:].bitcast(FP8X4), scales=plane[:], in_=a_lead_grouped[n][:].rearrange("p c t -> p (c t)")
            )
            a_mx[LEAD, n] = (codes[:].bitcast(FP8X4), plane[:])


        def copy_wide(values, name):
            wide = keep.tile([P, CHUNK], F32, name=name)
            nc.scalar.copy(out=wide[:].rearrange("q (p c) -> q p c", c=4), in_=values)
            return wide

        def spread_chunk(n, tag):
            bank = psum.tile([P, 4, P], F32, name="spread", tag=tag)
            for c in range(4):
                column = pair_words[:, 4 * n + c : 4 * n + c + 1].to_broadcast([P, P])
                nc.tensor.transpose(bank[:, c, :], column, identity[:])
            pairs = bank[:].rearrange("q c p -> q (c p)").bitcast(BF16).rearrange("q (c p e) -> q e p c", c=4, e=2)
            load_wide[n] = copy_wide(pairs[:, 0], "load_wide_%d" % n)
            if n % 2 == 1:
                dinv_psum[n] = pairs[:, 1]
            if n < CHUNKS - 1:
                dinv_sbuf[n] = copy_wide(pairs[:, 1], "dinv_wide_%d" % n)[:].rearrange("q (p c) -> q p c", c=4)


        def acc_tag(m, n):
            if (m, n) == (2, 0):
                return "spare"
            order = m + 2 * n if m < 2 and n < 2 else 2 * m + n % 2 - 1
            return "acc_%d" % (order % ACC_BANKS)

        def multiply_cols(bank, m, n, g, first, width):
            nc.tensor.matmul_mx(
                out=bank,
                lhsT=c_mx[m, g][0],
                lhsT_scale=c_mx[m, g][1],
                rhs=a_mx[g, n][0][:, first : first + width],
                rhs_scale=a_mx[g, n][1][:, first : first + width],
                start=(g == 0),
                stop=(g == LEAD),
            )

        def multiply(g, blocks):
            for m, n in blocks:
                if g == 0:
                    acc[m, n] = psum.tile([P, CHUNK], F32, name="acc", tag=acc_tag(m, n))
                multiply_cols(acc[m, n][:], m, n, g, 0, CHUNK)

        def multiply_block(m, n):
            for g in range(PASSES):
                multiply(g, [(m, n)])


        def result_cols(m, n, first, width):
            sweep, j = divmod(n, 2)
            if (m, sweep) not in result:
                result[m, sweep] = keep.tile([P, SWEEP], F32, name="result_%d_%d" % (m, sweep))
            return result[m, sweep][:, j * CHUNK + first : j * CHUNK + first + width]

        def residual_from(bank, m, n, first, width):
            nc.vector.scalar_tensor_tensor(
                out=result_cols(m, n, first, width),
                in0=bank,
                scalar=neg_kappa[:, m : m + 1],
                in1=load_wide[n][:, first : first + width],
                op0=ALU.mult,
                op1=ALU.add,
            )

        def residual(m, n, first=0, width=CHUNK):
            residual_from(acc[m, n][:, first : first + width], m, n, first, width)

        def scale(engine, table, m, n, first, width):
            cols = result_cols(m, n, first, width).rearrange("q (p c) -> q p c", c=4)
            engine.tensor_tensor(out=cols, in0=cols, in1=table[n][:, first // 4 : (first + width) // 4, :], op=ALU.mult)

        def scale_on_vector(m, n, first=0, width=CHUNK):
            scale(nc.vector, dinv_psum, m, n, first, width)

        def scale_on_gpsimd(m, n, first=0, width=CHUNK):
            scale(nc.gpsimd, dinv_sbuf, m, n, first, width)

        def store_first_sweep(m):
            nc.sync.dma_start(out=out_rows[:, m, :SWEEP], in_=result[m, 0][:])

        def store(m, n, first=0, width=CHUNK):
            start = n * CHUNK + first
            nc.sync.dma_start(out=out_rows[:, m, start : start + width], in_=result_cols(m, n, first, width))

        clear_tail_scales(0)
        clear_tail_scales(1)
        identity = keep.tile([P, P], F32)
        make_identity(nc, identity[:])
        load_in = keep.tile([P, CHUNKS, 4], BF16)
        dinv_in = keep.tile([P, CHUNKS, 4], BF16)
        kappa_in = keep.tile([P, ROW_TILES], BF16)
        load_c_tail(0)
        nc.scalar.dma_start(out=load_in[:], in_=load.rearrange("(n p c) -> p n c", n=CHUNKS, c=4))
        nc.scalar.dma_start(out=dinv_in[:], in_=dinv.rearrange("(n p c) -> p n c", n=CHUNKS, c=4))
        nc.gpsimd.dma_start(out=kappa_in[:], in_=kappa.rearrange("(p m) -> p m", m=ROW_TILES))
        load_tail_scales(0)
        load_tail_codes(0, 0, 1)
        load_tail_codes(0, 1, 1)
        load_c_tail(1)
        load_tail_codes(0, 2, 1)
        load_c_lead(0)
        load_a_lead(0)
        load_c_tail(2)
        load_c_lead(2)
        load_a_lead(1)
        load_c_tail(3)
        load_c_tail(4)
        load_c_lead(4)
        load_a_lead(2)
        load_c_tail(5)
        load_a_lead(3)
        load_c_tail(6)
        load_c_lead(6)
        load_c_tail(7)
        load_tail_scales(1)
        load_tail_codes(1, 0, TAIL_PASSES)

        pairs_in = keep.tile([P, 4 * CHUNKS, 2], BF16)
        nc.vector.tensor_copy(out=pairs_in[:, :, 0], in_=load_in[:].rearrange("p n c -> p (n c)"))
        nc.vector.tensor_copy(out=pairs_in[:, :, 1], in_=dinv_in[:].rearrange("p n c -> p (n c)"))
        pair_words = pairs_in[:].rearrange("p a e -> p (a e)").bitcast(F32)

        for key in ((0, "tail"), (1, "tail"), (0, "lead")):
            take_stepped(key)
        prepare_items([(0, 0)], "turned_0")
        prepare_items([(0, 1), (0, 2)], "turned_1")
        spread_chunk(0, "spare")
        spread_chunk(1, "held")
        multiply(0, [(0, 0), (0, 1)])
        multiply(1, [(0, 0), (0, 1)])
        prepare_items([(1, 0), (1, 1)], "turned_0")
        prepare_items([(1, 2)], "turned_1")
        multiply(2, [(0, 0), (0, 1)])
        lead_items = [(0, LEAD), (1, LEAD)]
        lead_bank = turn(lead_items, "spare")
        multiply(0, [(1, 0), (1, 1)])
        multiply(1, [(1, 0), (1, 1)])
        sort_words((2, "tail"))
        sort_words((2, "lead"))
        lead_grouped = copy_turned(lead_bank)
        group_a_lead(0, nc.vector.tensor_copy, 0, CHUNK)
        neg_kappa = keep.tile([P, ROW_TILES], F32)
        nc.vector.tensor_scalar(out=neg_kappa[:], in0=kappa_in[:], scalar1=-1.0, scalar2=None, op0=ALU.mult)
        quantize_a_lead(0)
        quantize_c(lead_items, lead_grouped)
        group_a_lead(1, nc.vector.tensor_copy, 0, HALF_CHUNK)
        prepare_items([(2, 0), (2, 1)], "turned_0")
        prepare_items([(2, 2), (2, LEAD)], "turned_1")
        multiply(2, [(1, 0), (1, 1)])
        multiply(LEAD, [(0, 0), (1, 0)])
        multiply_block(2, 0)
        group_a_lead(1, nc.vector.tensor_copy, HALF_CHUNK, HALF_CHUNK)
        residual(0, 0)
        quantize_a_lead(1)
        residual(1, 0)
        sort_words((3, "tail"))
        sort_words((4, "tail"))
        sort_words((4, "lead"))
        grouped = turn_row_tile(3)
        sort_words((5, "tail"))
        for g in range(TAIL_PASSES):
            multiply(g, [(2, 1)])
        multiply(LEAD, [(0, 1), (1, 1), (2, 1)])
        quantize_row_tile(3, grouped)
        residual(2, 0)
        scale_on_gpsimd(2, 0)
        residual(0, 1)
        residual(1, 1)

        for m in range(HEAD_TILES, ROW_TILES):
            if m + 1 <= LAST:
                grouped = turn_row_tile(m + 1)
            if m + 3 <= LAST:
                sort_words((m + 3, "tail"))
                if (m + 3) % 2 == 0:
                    sort_words((m + 3, "lead"))
            if m + 1 in (LAST - 1, LAST):
                spread_chunk(m + 1 - LAST + 3, "spare")
            n, half = divmod(m, 2)
            if m > HEAD_TILES and m + 1 != LAST - 1:
                group_a_lead(n, nc.scalar.copy, half * HALF_CHUNK, HALF_CHUNK)
            residual(m - 1, 1)
            multiply_block(m, 0)
            if m + 1 <= LAST:
                quantize_row_tile(m + 1, grouped)
            if m + 1 == LAST - 1:
                group_a_lead(n, nc.vector.tensor_copy, half * HALF_CHUNK, HALF_CHUNK)
            if m >= LAST - 1:
                quantize_a_lead(m - LAST + 3)
            residual(m, 0)
            scale_on_gpsimd(m, 0)
            scale_on_vector(m - 1, 1)
            store_first_sweep(m - 1)
            multiply_block(m, 1)

        late_blocks = [(m, n) for m in range(2) for n in range(2)]

        def finish_late(s):
            scale_on_gpsimd(*late_blocks[s])
            store(*late_blocks[s])

        finish_late(0)
        residual(LAST, 1)

        for m in range(LAST):
            multiply_block(m, 2)
            residual(m, 2)
            scale_on_gpsimd(m, 2)
            if m == 0:
                scale_on_vector(LAST, 1)
                store_first_sweep(LAST)
            else:
                scale_on_vector(m - 1, 3)
                store(m - 1, 3)
            store(m, 2)
            if m + 1 < len(late_blocks):
                finish_late(m + 1)
            multiply_block(m, 3)
            if m < LAST - 1:
                residual(m, 3)

        halves = (0, HALF_CHUNK)
        for first in halves:
            residual(LAST - 1, 3, first, HALF_CHUNK)
        for first in halves:
            scale_on_vector(LAST - 1, 3, first, HALF_CHUNK)
        store(LAST - 1, 3)
        multiply_block(LAST, 2)
        for first in halves:
            residual(LAST, 2, first, HALF_CHUNK)
            scale_on_gpsimd(LAST, 2, first, HALF_CHUNK)
        store(LAST, 2, 0, HALF_CHUNK)
        for first, width, tag in ((0, 2 * P, "turned_0"), (2 * P, P, "turned_1"), (3 * P, P, "held")):
            bank = psum.tile([P, width], F32, name="piece", tag=tag)
            for start in range(0, width, P):
                for g in range(PASSES):
                    multiply_cols(bank[:, start : start + P], LAST, 3, g, first + start, P)
            residual_from(bank[:], LAST, 3, first, width)
            if first == HALF_CHUNK:
                scale_on_vector(LAST, 3, 0, HALF_CHUNK)
                store(LAST, 3, 0, HALF_CHUNK)
        store(LAST, 2, HALF_CHUNK, HALF_CHUNK)
        for first in (2 * P, 3 * P):
            scale_on_vector(LAST, 3, first, P)
        store(LAST, 3, HALF_CHUNK, HALF_CHUNK)
